import numpy as np
import ml_dtypes


def mxq(x, axis, fmt="e4m3"):
    dtype, down = {"e4m3": (ml_dtypes.float8_e4m3fn, 7), "e5m2": (ml_dtypes.float8_e5m2, 14)}[fmt]
    v = np.moveaxis(np.asarray(x, np.float32).astype(ml_dtypes.bfloat16).astype(np.float64), axis, -1)
    blocks = v.reshape(v.shape[:-1] + (-1, 32))
    amax = np.abs(blocks).max(-1, keepdims=True)
    byte = np.maximum(np.where(amax > 0, np.frexp(amax)[1] - 1 + 127, 0) - down, 1)
    scale = np.exp2(byte - 127.0)
    codes = (blocks / scale).astype(np.float32).astype(dtype).astype(np.float64)
    return np.moveaxis((codes * scale).reshape(v.shape), -1, axis)


WIDE = False


def mx_kscale(k):
    if not WIDE:
        return np.ones(k)
    levels = np.array([10, -10, 5, -5, 0])
    if k % 512:
        return np.exp2(np.random.permutation(np.resize(levels, k // 32))).repeat(32)
    a = np.empty((k // 512, 16))
    for p in range(k // 512):
        a[p, :8] = np.random.permutation(np.resize(levels, 8))
        for g in range(8):
            far = levels[np.abs(levels - a[p, g]) >= 10]
            a[p, g + 8] = far[np.random.randint(len(far))]
    return np.exp2(a.ravel()).repeat(32)


def f64(x):
    return np.asarray(x).astype(np.float64)


def striped(idx):
    return np.tile(idx.reshape(-1, 16).T, (8, 1)).astype(np.uint16)


def unstriped(offs):
    return offs[:16].T.reshape(-1).astype(np.int64)


def silu(v):
    return v / (1.0 + np.exp(-np.maximum(v, -700.0)))


K, T, E, C, H, N = 1536, 1024, 4, 128, 512, 256


def by_expert(wq, xq):
    return np.concatenate([wq[e].T @ xq[:, e * C:(e + 1) * C] for e in range(E)], axis=1)


def setup_inputs():
    n = np.random.standard_normal
    s = mx_kscale(K)[:, None]
    u = mx_kscale(H)
    return {
        "xT": (n((K, T)) * s).astype(np.float32),
        "w1": (n((E, K, H)) / np.sqrt(K) / s[None]).astype(np.float32),
        "w3": (n((E, K, H)) / np.sqrt(K) / s[None] * u[None, None, :]).astype(np.float32),
        "w2": (n((E, H, N)) / np.sqrt(H) / u[None, :, None]).astype(np.float32),
        "gate": np.tile(np.random.uniform(0.2, 1.0, E * C), (N, 1)).astype(np.float32),
        "offs": striped(np.random.permutation(T)[:E * C]),
    }


def reference(xT, w1, w3, w2, gate, offs):
    idx = unstriped(offs)
    xq = mxq(f64(xT)[:, idx], 0, "e4m3")
    h = silu(by_expert(mxq(f64(w1), 1, "e4m3"), xq))
    h = h * by_expert(mxq(f64(w3), 1, "e4m3"), xq)
    y = by_expert(mxq(f64(w2), 1, "e4m3"), mxq(h, 0, "e4m3"))
    out = np.zeros((N, T))
    out[:, idx] = f64(gate) * y
    return out

@@ -1,0 +1,217 @@
+from contextlib import ExitStack
+
+import concourse.mybir as mybir
+
+K, T, E, C, H, N = 1536, 1024, 4, 128, 512, 256
+S = E * C
+P = 128
+J = 4
+G = K // (P * J)
+NB = N // P
+
+F32 = mybir.dt.float32
+BF16 = mybir.dt.bfloat16
+U32 = mybir.dt.uint32
+U16 = mybir.dt.uint16
+U8 = mybir.dt.uint8
+FP8X4 = mybir.dt.float8_e4m3fn_x4
+MULT = mybir.AluOpType.mult
+SILU = mybir.ActivationFunctionType.Silu
+
+V_M_LAST = 72
+
+FLOPS = 2 * S * (2 * K * H + H * N)
+
+
+def flat(grouped):
+    return grouped.rearrange("p w j -> p (w j)")
+
+
+def tile_routed_moe_kernel(tc, xT, w1, w3, w2, gate, offs, out):
+    nc = tc.nc
+    x_rows = xT.rearrange("(g p j) n -> g p (j n)", p=P, j=J)
+    w_rows = [w.rearrange("e (g p j) h -> e g p (j h)", p=P, j=J) for w in (w1, w3)]
+    w2_rows = w2.rearrange("e (p j) n -> e p (j n)", j=J)
+
+    with ExitStack() as ctx:
+        keep = ctx.enter_context(tc.tile_pool(name="keep", bufs=1))
+        xrawp = ctx.enter_context(tc.tile_pool(name="xrawp", bufs=3))
+        rawp = ctx.enter_context(tc.tile_pool(name="rawp", bufs=7))
+        grpp = ctx.enter_context(tc.tile_pool(name="grpp", bufs=3))
+        grpv = ctx.enter_context(tc.tile_pool(name="grpv", bufs=2))
+        wq = ctx.enter_context(tc.tile_pool(name="wq", bufs=2))
+        work = ctx.enter_context(tc.tile_pool(name="work", bufs=2))
+        psum = ctx.enter_context(tc.psum_pool(name="psum", bufs=2))
+
+        lst = keep.tile([P, S // 16], U16, name="lst")
+        gt = keep.tile([P, NB, S], F32, name="gt")
+        wins = []
+        for b in range(NB):
+            win = keep.tile([P, T], F32, name=f"win{b}")
+            nc.vector.memset(win[:], 0.0)
+            wins.append(win)
+        warm = keep.tile([P, 1], F32, name="warm")
+        nc.vector.memset(warm[:], 0.0)
+        nc.scalar.activation(warm[:], warm[:], SILU)
+
+        gw = keep.tile([P, G, S], U32, name="gw", align_bytes=64)
+        gs = keep.tile([P, G, S], U8, name="gs", align_bytes=64)
+        for g in range(G):
+            xraw = xrawp.tile([P, J * T], F32, name="xraw")
+            nc.sync.dma_start(xraw[:], x_rows[g])
+            if g == 0:
+                nc.sync.dma_start(lst[:], offs)
+            xin = xraw[:].rearrange("p (j c i) -> p c j i", j=J, i=4)
+            xw = keep.tile([P, T], U32, name=f"xw{g}", align_bytes=64)
+            xs = keep.tile([P, T], U8, name=f"xs{g}", align_bytes=64)
+            for half in range(2):
+                t0 = half * H
+                cols = slice(t0, t0 + H)
+                if (g, half) in ((0, 0), (2, 0)):
+                    grp = grpv.tile([P, H, J], BF16, name="grp_v", align_bytes=64)
+                    nc.vector.tensor_copy(grp[:].rearrange("p (c i) j -> p c j i", i=4), xin[:, t0 // 4:t0 // 4 + H // 4])
+                else:
+                    grp = grpp.tile([P, H, J], BF16, name="grp_s", align_bytes=64)
+                    nc.scalar.copy(grp[:].rearrange("p (c i) j -> p c j i", i=4), xin[:, t0 // 4:t0 // 4 + H // 4])
+                nc.vector.quantize_mx(out=xw[:, cols].bitcast(FP8X4), scales=xs[:, cols], in_=flat(grp[:]))
+            nc.vector.tensor_copy(gw[:, g, :], xw[:].indirect(lst[:]))
+            nc.vector.tensor_copy(gs[:, g, :], xs[:].indirect(lst[:]))
+
+        state = {}
+
+        def slots(e):
+            return slice(C * e, C * e + C)
+
+        def first_layer(e, which):
+            wc, ws = state["w", e, which]
+            acc = psum.tile([P, 4, C], F32, name=f"acc{which}")
+            for t in range(4):
+                for g in range(G):
+                    nc.tensor.matmul_mx(
+                        out=acc[:, t, :],
+                        lhsT=wc[:, g, P * t:P * t + P].bitcast(FP8X4),
+                        lhsT_scale=ws[:, g, P * t:P * t + P],
+                        rhs=gw[:, g, slots(e)].bitcast(FP8X4),
+                        rhs_scale=gs[:, g, slots(e)],
+                        start=(g == 0),
+                        stop=(g == G - 1),
+                    )
+            state["acc", e, which] = acc
+
+        def silu(e):
+            sil = work.tile([P, 4, C], F32, name="sil")
+            nc.scalar.activation(sil[:], state["acc", e, 0][:], SILU)
+            state["sil", e] = sil
+
+        def product(e):
+            hb = work.tile([P, C, 4], BF16, name="hb", align_bytes=64)
+            nc.vector.tensor_tensor(hb[:], state["sil", e][:].rearrange("p t c -> p c t"), state["acc", e, 1][:].rearrange("p t c -> p c t"), MULT)
+            state["hb", e] = hb
+
+        def quantise_hidden(e):
+            hc = work.tile([P, C], U32, name="hc", align_bytes=64)
+            hs = work.tile([P, C], U8, name="hs", align_bytes=64)
+            nc.vector.quantize_mx(out=hc[:].bitcast(FP8X4), scales=hs[:], in_=flat(state["hb", e][:]))
+            vc, vs = state["w2", e]
+            y = psum.tile([P, NB, C], F32, name="y")
+            for b in range(NB):
+                nc.tensor.matmul_mx(
+                    out=y[:, b, :],
+                    lhsT=vc[:, P * b:P * b + P].bitcast(FP8X4),
+                    lhsT_scale=vs[:, P * b:P * b + P],
+                    rhs=hc[:].bitcast(FP8X4),
+                    rhs_scale=hs[:],
+                    start=True,
+                    stop=True,
+                )
+            state["y", e] = y
+
+        def gated(e):
+            yg = work.tile([P, NB, C], F32, name="yg")
+            nc.vector.tensor_tensor(yg[:], state["y", e][:], gt[:, :, slots(e)], MULT)
+            state["yg", e] = yg
+
+        def scatter(e, b):
+            nc.vector.tensor_copy(wins[b][:].indirect(lst[:, 8 * e:8 * e + 8]), state["yg", e][:, b, :])
+
+        items = []
+        for e in range(E):
+            items.extend([(e, which, g) for which in range(2) for g in range(G)])
+            items.append((e, 2, 0))
+        later = []
+        pending = []
+        for step, (e, which, g) in enumerate(items):
+            last = e == E - 1
+            if last and which == 2:
+                for codes, scales, grouped in pending:
+                    nc.vector.quantize_mx(out=codes.bitcast(FP8X4), scales=scales, in_=flat(grouped))
+            if which == 2:
+                raw = work.tile([P, J * N], F32, name="raw2")
+                nc.sync.dma_start(raw[:], w2_rows[e])
+                if e == 0:
+                    nc.sync.dma_start(gt[:], gate.rearrange("(b p) s -> p b s", p=P))
+                grp = work.tile([P, N, J], BF16, name="grp2", align_bytes=64)
+                n0 = N // 8 if last else 0
+                src = raw[:].rearrange("p (j c i) -> p c j i", j=J, i=4)
+                dst = grp[:].rearrange("p (c i) j -> p c j i", i=4)
+                if last:
+                    nc.vector.tensor_copy(dst[:, :n0], src[:, :n0])
+                nc.scalar.copy(dst[:, n0:], src[:, n0:])
+                vc = work.tile([P, N], U32, name="vc", align_bytes=64)
+                vs = work.tile([P, N], U8, name="vs", align_bytes=64)
+                state["w2", e] = (vc, vs)
+                jobs = [(vc[:], vs[:], grp[:])]
+            else:
+                final = last and which == 1 and g == G - 1
+                raw = rawp.tile([P, J * H], F32, name="raw")
+                pieces = 2 if final else 1
+                for q in range(pieces):
+                    part = slice(q * J * H // pieces, (q + 1) * J * H // pieces)
+                    nc.sync.dma_start(raw[:, part], w_rows[which][e, g, :, part])
+                if g == 0:
+                    wc = wq.tile([P, G, H], U32, name=f"wc{which}", align_bytes=64)
+                    ws = wq.tile([P, G, H], U8, name=f"ws{which}", align_bytes=64)
+                    state["w", e, which] = (wc, ws)
+                wc, ws = state["w", e, which]
+                on_v = (G * which + g) in ((1, 4, 5), (1, 4, 5), (1, 4, 5), (1, 4, 5))[e]
+                grp = grpv.tile([P, H, J], BF16, name="grp_v", align_bytes=64) if on_v else grpp.tile([P, H, J], BF16, name="grp_s", align_bytes=64)
+                src = raw[:].rearrange("p (j m t) -> p m j t", j=J, t=4)
+                dst = grp[:].rearrange("p (t m) j -> p m j t", t=4)
+                m = (V_M_LAST if final else P) if on_v else 0
+                for q in range(pieces):
+                    js = slice(q * J // pieces, (q + 1) * J // pieces)
+                    if m:
+                        nc.vector.tensor_copy(dst[:, :m, js, :], src[:, :m, js, :])
+                    if m < P:
+                        nc.scalar.copy(dst[:, m:, js, :], src[:, m:, js, :])
+                parts = 2 if final else 1
+                width = H // parts
+                jobs = [(wc[:, g, u * width:u * width + width], ws[:, g, u * width:u * width + width], grp[:, u * width:u * width + width, :]) for u in range(parts)]
+            if not (last and which == 2):
+                for codes, scales, grouped in pending:
+                    nc.vector.quantize_mx(out=codes.bitcast(FP8X4), scales=scales, in_=flat(grouped))
+            pending = jobs
+            for due, function, args in later:
+                if due == step:
+                    function(*args)
+            if which < 2 and g == G - 1:
+                later.append((step + 1, first_layer, (e, which)))
+                if which == 0:
+                    later.append((step + 3, silu, (e,)))
+                elif not last:
+                    later.append((step + 2, product, (e,)))
+                    later.append((step + 3, quantise_hidden, (e,)))
+                    later.append((step + 4, gated, (e,)))
+                    later.append((step + 5, scatter, (e, 0)))
+                    later.append((step + 6, scatter, (e, 1)))
+        for codes, scales, grouped in pending:
+            nc.vector.quantize_mx(out=codes.bitcast(FP8X4), scales=scales, in_=flat(grouped))
+        e = E - 1
+        product(e)
+        quantise_hidden(e)
+        yg = work.tile([P, NB, C], F32, name="yg")
+        for b in range(NB):
+            nc.vector.tensor_tensor(yg[:, b, :], state["y", e][:, b, :], gt[:, b, slots(e)], MULT)
+            state["yg", e] = yg
+            scatter(e, b)
+            nc.sync.dma_start(out[P * b:P * b + P, :], wins[b][:])

@@ -18,7 +18,8 @@ FP8X4 = mybir.dt.float8_e4m3fn_x4
 MULT = mybir.AluOpType.mult
 SILU = mybir.ActivationFunctionType.Silu
 
-V_M_LAST = 72
+WHOLE = 0
+V_SHARE = ((0, 128, 0, 0, 128, 128), (0, 128, 0, 0, 128, 128), (0, 128, 0, 0, 128, 64), (64, 0, 48, 48, 88, 88))
 
 FLOPS = 2 * S * (2 * K * H + H * N)
 
@@ -30,21 +31,26 @@ def flat(grouped):
 def tile_routed_moe_kernel(tc, xT, w1, w3, w2, gate, offs, out):
     nc = tc.nc
     x_rows = xT.rearrange("(g p j) n -> g p (j n)", p=P, j=J)
-    w_rows = [w.rearrange("e (g p j) h -> e g p (j h)", p=P, j=J) for w in (w1, w3)]
-    w2_rows = w2.rearrange("e (p j) n -> e p (j n)", j=J)
+    w_rows = [w.rearrange("e (g p j) h -> e p g (j h)", p=P, j=J) for w in (w1, w3)]
+    w2_rows = w2.rearrange("e (p j) n -> p e (j n)", j=J)
+    gate_rows = gate.rearrange("(b p) s -> p b s", p=P)
 
     with ExitStack() as ctx:
         keep = ctx.enter_context(tc.tile_pool(name="keep", bufs=1))
-        xrawp = ctx.enter_context(tc.tile_pool(name="xrawp", bufs=3))
-        rawp = ctx.enter_context(tc.tile_pool(name="rawp", bufs=7))
+        rawp = ctx.enter_context(tc.tile_pool(name="rawp", bufs=5))
         grpp = ctx.enter_context(tc.tile_pool(name="grpp", bufs=3))
         grpv = ctx.enter_context(tc.tile_pool(name="grpv", bufs=2))
         wq = ctx.enter_context(tc.tile_pool(name="wq", bufs=2))
         work = ctx.enter_context(tc.tile_pool(name="work", bufs=2))
+        turn = ctx.enter_context(tc.tile_pool(name="turn", bufs=1))
         psum = ctx.enter_context(tc.psum_pool(name="psum", bufs=2))
 
+        def quantise(codes, scales, grouped):
+            nc.vector.quantize_mx(out=codes.bitcast(FP8X4), scales=scales, in_=flat(grouped))
+
         lst = keep.tile([P, S // 16], U16, name="lst")
-        gt = keep.tile([P, NB, S], F32, name="gt")
+        gt = keep.tile([P, NB, S - C], F32, name="gt")
+        raw2 = keep.tile([P, E - 1, J * N], F32, name="raw2")
         wins = []
         for b in range(NB):
             win = keep.tile([P, T], F32, name=f"win{b}")
@@ -55,15 +61,15 @@ def tile_routed_moe_kernel(tc, xT, w1, w3, w2, gate, offs, out):
         nc.scalar.activation(warm[:], warm[:], SILU)
 
         gw = keep.tile([P, G, S], U32, name="gw", align_bytes=64)
-        gs = keep.tile([P, G, S], U8, name="gs", align_bytes=64)
+        gs = keep.tile([P, S], U8, name="gs", align_bytes=64)
+        xs = keep.tile([P, T], U8, name="xs", align_bytes=64)
         for g in range(G):
-            xraw = xrawp.tile([P, J * T], F32, name="xraw")
+            xraw = rawp.tile([P, J * T], F32, name="raw")
             nc.sync.dma_start(xraw[:], x_rows[g])
             if g == 0:
                 nc.sync.dma_start(lst[:], offs)
             xin = xraw[:].rearrange("p (j c i) -> p c j i", j=J, i=4)
             xw = keep.tile([P, T], U32, name=f"xw{g}", align_bytes=64)
-            xs = keep.tile([P, T], U8, name=f"xs{g}", align_bytes=64)
             for half in range(2):
                 t0 = half * H
                 cols = slice(t0, t0 + H)
@@ -73,45 +79,45 @@ def tile_routed_moe_kernel(tc, xT, w1, w3, w2, gate, offs, out):
                 else:
                     grp = grpp.tile([P, H, J], BF16, name="grp_s", align_bytes=64)
                     nc.scalar.copy(grp[:].rearrange("p (c i) j -> p c j i", i=4), xin[:, t0 // 4:t0 // 4 + H // 4])
-                nc.vector.quantize_mx(out=xw[:, cols].bitcast(FP8X4), scales=xs[:, cols], in_=flat(grp[:]))
+                quantise(xw[:, cols], xs[4 * g:, cols], grp[:])
             nc.vector.tensor_copy(gw[:, g, :], xw[:].indirect(lst[:]))
-            nc.vector.tensor_copy(gs[:, g, :], xs[:].indirect(lst[:]))
+        nc.vector.tensor_copy(gs[:], xs[:].indirect(lst[:]))
 
         state = {}
 
         def slots(e):
             return slice(C * e, C * e + C)
 
-        def first_layer(e, which):
+        def first_layer(e, which, g, tiles):
             wc, ws = state["w", e, which]
-            acc = psum.tile([P, 4, C], F32, name=f"acc{which}")
-            for t in range(4):
-                for g in range(G):
-                    nc.tensor.matmul_mx(
-                        out=acc[:, t, :],
-                        lhsT=wc[:, g, P * t:P * t + P].bitcast(FP8X4),
-                        lhsT_scale=ws[:, g, P * t:P * t + P],
-                        rhs=gw[:, g, slots(e)].bitcast(FP8X4),
-                        rhs_scale=gs[:, g, slots(e)],
-                        start=(g == 0),
-                        stop=(g == G - 1),
-                    )
-            state["acc", e, which] = acc
+            if g == 0:
+                state["acc", e, which] = psum.tile([P, 4, C], F32, name=f"acc{which}")
+            acc = state["acc", e, which]
+            for t in tiles:
+                nc.tensor.matmul_mx(
+                    out=acc[:, t, :],
+                    lhsT=wc[:, g, P * t:P * t + P].bitcast(FP8X4),
+                    lhsT_scale=ws[:, g, P * t:P * t + P],
+                    rhs=gw[:, g, slots(e)].bitcast(FP8X4),
+                    rhs_scale=gs[4 * g:, slots(e)],
+                    start=(g == 0 and t == 0),
+                    stop=(g == G - 1 and t == 3),
+                )
 
         def silu(e):
-            sil = work.tile([P, 4, C], F32, name="sil")
+            sil = turn.tile([P, 4, C], F32, name="sil", align_bytes=64)
             nc.scalar.activation(sil[:], state["acc", e, 0][:], SILU)
             state["sil", e] = sil
 
         def product(e):
-            hb = work.tile([P, C, 4], BF16, name="hb", align_bytes=64)
+            hb = turn.tile([P, C, 4], BF16, name="odd" if e == E - 2 else "hb", align_bytes=64)
             nc.vector.tensor_tensor(hb[:], state["sil", e][:].rearrange("p t c -> p c t"), state["acc", e, 1][:].rearrange("p t c -> p c t"), MULT)
             state["hb", e] = hb
 
-        def quantise_hidden(e):
+        def second_layer(e):
             hc = work.tile([P, C], U32, name="hc", align_bytes=64)
             hs = work.tile([P, C], U8, name="hs", align_bytes=64)
-            nc.vector.quantize_mx(out=hc[:].bitcast(FP8X4), scales=hs[:], in_=flat(state["hb", e][:]))
+            quantise(hc[:], hs[:], state["hb", e][:])
             vc, vs = state["w2", e]
             y = psum.tile([P, NB, C], F32, name="y")
             for b in range(NB):
@@ -127,91 +133,103 @@ def tile_routed_moe_kernel(tc, xT, w1, w3, w2, gate, offs, out):
             state["y", e] = y
 
         def gated(e):
-            yg = work.tile([P, NB, C], F32, name="yg")
+            yg = turn.tile([P, NB, C], F32, name="even" if e == E - 2 else "yg", align_bytes=64)
             nc.vector.tensor_tensor(yg[:], state["y", e][:], gt[:, :, slots(e)], MULT)
             state["yg", e] = yg
 
         def scatter(e, b):
             nc.vector.tensor_copy(wins[b][:].indirect(lst[:, 8 * e:8 * e + 8]), state["yg", e][:, b, :])
 
+        def interleave_w2(e, raw, grp):
+            nc.scalar.copy(grp.rearrange("p (c i) j -> p c j i", i=4), raw.rearrange("p (j c i) -> p c j i", j=J, i=4))
+            vc = turn.tile([P, N], U32, name="sil", align_bytes=64) if e == E - 1 else work.tile([P, N], U32, name="vc", align_bytes=64)
+            vs = work.tile([P, N], U8, name="vs", align_bytes=64)
+            state["w2", e] = (vc, vs)
+            return (vc[:], vs[:], grp)
+
+        def interleave(grp, raw, m, js):
+            src = raw.rearrange("p (j m t) -> p m j t", j=J, t=4)
+            dst = grp.rearrange("p (t m) j -> p m j t", t=4)
+            if m:
+                nc.vector.tensor_copy(dst[:, :m, js, :], src[:, :m, js, :])
+            if m < P:
+                nc.scalar.copy(dst[:, m:, js, :], src[:, m:, js, :])
+
         items = []
         for e in range(E):
             items.extend([(e, which, g) for which in range(2) for g in range(G)])
             items.append((e, 2, 0))
         later = []
-        pending = []
-        for step, (e, which, g) in enumerate(items):
-            last = e == E - 1
-            if last and which == 2:
-                for codes, scales, grouped in pending:
-                    nc.vector.quantize_mx(out=codes.bitcast(FP8X4), scales=scales, in_=flat(grouped))
+        pending = None
+        for step, (e, which, g) in enumerate(items[:-2]):
             if which == 2:
-                raw = work.tile([P, J * N], F32, name="raw2")
-                nc.sync.dma_start(raw[:], w2_rows[e])
                 if e == 0:
-                    nc.sync.dma_start(gt[:], gate.rearrange("(b p) s -> p b s", p=P))
+                    nc.sync.dma_start(raw2[:], w2_rows[:, :E - 1])
+                    nc.sync.dma_start(gt[:], gate_rows[:, :, :S - C])
                 grp = work.tile([P, N, J], BF16, name="grp2", align_bytes=64)
-                n0 = N // 8 if last else 0
-                src = raw[:].rearrange("p (j c i) -> p c j i", j=J, i=4)
-                dst = grp[:].rearrange("p (c i) j -> p c j i", i=4)
-                if last:
-                    nc.vector.tensor_copy(dst[:, :n0], src[:, :n0])
-                nc.scalar.copy(dst[:, n0:], src[:, n0:])
-                vc = work.tile([P, N], U32, name="vc", align_bytes=64)
-                vs = work.tile([P, N], U8, name="vs", align_bytes=64)
-                state["w2", e] = (vc, vs)
-                jobs = [(vc[:], vs[:], grp[:])]
+                job = interleave_w2(e, raw2[:, e], grp[:])
             else:
-                final = last and which == 1 and g == G - 1
-                raw = rawp.tile([P, J * H], F32, name="raw")
-                pieces = 2 if final else 1
-                for q in range(pieces):
-                    part = slice(q * J * H // pieces, (q + 1) * J * H // pieces)
-                    nc.sync.dma_start(raw[:, part], w_rows[which][e, g, :, part])
                 if g == 0:
+                    raw = rawp.tile([P, G, J * H], F32, name="raw")
                     wc = wq.tile([P, G, H], U32, name=f"wc{which}", align_bytes=64)
                     ws = wq.tile([P, G, H], U8, name=f"ws{which}", align_bytes=64)
                     state["w", e, which] = (wc, ws)
-                wc, ws = state["w", e, which]
-                on_v = (G * which + g) in ((1, 4, 5), (1, 4, 5), (1, 4, 5), (1, 4, 5))[e]
-                grp = grpv.tile([P, H, J], BF16, name="grp_v", align_bytes=64) if on_v else grpp.tile([P, H, J], BF16, name="grp_s", align_bytes=64)
-                src = raw[:].rearrange("p (j m t) -> p m j t", j=J, t=4)
-                dst = grp[:].rearrange("p (t m) j -> p m j t", t=4)
-                m = (V_M_LAST if final else P) if on_v else 0
-                for q in range(pieces):
-                    js = slice(q * J // pieces, (q + 1) * J // pieces)
-                    if m:
-                        nc.vector.tensor_copy(dst[:, :m, js, :], src[:, :m, js, :])
-                    if m < P:
-                        nc.scalar.copy(dst[:, m:, js, :], src[:, m:, js, :])
-                parts = 2 if final else 1
-                width = H // parts
-                jobs = [(wc[:, g, u * width:u * width + width], ws[:, g, u * width:u * width + width], grp[:, u * width:u * width + width, :]) for u in range(parts)]
-            if not (last and which == 2):
-                for codes, scales, grouped in pending:
-                    nc.vector.quantize_mx(out=codes.bitcast(FP8X4), scales=scales, in_=flat(grouped))
-            pending = jobs
+                if 2 * e + which >= WHOLE:
+                    nc.sync.dma_start(raw[:, g], w_rows[which][e, :, g])
+                elif g == 0:
+                    nc.sync.dma_start(raw[:], w_rows[which][e])
+                m = V_SHARE[e][G * which + g]
+                if e == E - 1 and G * which + g > 0:
+                    grp = turn.tile([P, H, J], BF16, name="odd" if (G * which + g) % 2 else "even", align_bytes=64)
+                elif m:
+                    grp = grpv.tile([P, H, J], BF16, name="grp_v", align_bytes=64)
+                else:
+                    grp = grpp.tile([P, H, J], BF16, name="grp_s", align_bytes=64)
+                interleave(grp[:], raw[:, g], m, slice(0, J))
+                job = (wc[:, g], ws[:, g], grp[:])
+            if pending:
+                quantise(*pending)
+            pending = job
             for due, function, args in later:
                 if due == step:
                     function(*args)
-            if which < 2 and g == G - 1:
-                later.append((step + 1, first_layer, (e, which)))
-                if which == 0:
-                    later.append((step + 3, silu, (e,)))
-                elif not last:
-                    later.append((step + 2, product, (e,)))
-                    later.append((step + 3, quantise_hidden, (e,)))
-                    later.append((step + 4, gated, (e,)))
-                    later.append((step + 5, scatter, (e, 0)))
-                    later.append((step + 6, scatter, (e, 1)))
-        for codes, scales, grouped in pending:
-            nc.vector.quantize_mx(out=codes.bitcast(FP8X4), scales=scales, in_=flat(grouped))
-        e = E - 1
+            if which < 2:
+                later.append((step + 1, first_layer, (e, which, g, range(4))))
+            if which == 0 and g == G - 1:
+                later.append((step + 2, silu, (e,)))
+            if which == 1 and g == G - 1:
+                later.append((step + 2, product, (e,)))
+                later.append((step + 2, second_layer, (e,)))
+                later.append((step + 3, gated, (e,)))
+                later.append((step + 3, scatter, (e, 0)))
+                later.append((step + 3, scatter, (e, 1)))
+
+        e, g = E - 1, G - 1
+        tail = rawp.tile([P, J * H + J * N + NB * C], F32, name="raw")
+        half = J * H // 2
+        for q in range(2):
+            nc.sync.dma_start(tail[:, q * half:q * half + half], w_rows[1][e, :, g, q * half:q * half + half])
+        nc.sync.dma_start(tail[:, J * H:J * H + J * N], w2_rows[:, e])
+        gt_last = tail[:, J * H + J * N:].rearrange("p (b s) -> p b s", b=NB)
+        nc.sync.dma_start(gt_last, gate_rows[:, :, S - C:])
+        quantise(*pending)
+        first_layer(e, 1, g - 1, range(4))
+        grp = turn.tile([P, H + N, J], BF16, name="even", align_bytes=64)
+        m = V_SHARE[e][-1]
+        interleave(grp[:, :H], tail[:, :J * H], m, slice(0, 2))
+        interleave(grp[:, :H], tail[:, :J * H], m, slice(2, 4))
+        for u in range(2):
+            cols = slice(u * H // 2, (u + 1) * H // 2)
+            quantise(wc[:, g, cols], ws[:, g, cols], grp[:, cols, :])
+            first_layer(e, 1, g, range(2 * u, 2 * u + 2))
         product(e)
-        quantise_hidden(e)
-        yg = work.tile([P, NB, C], F32, name="yg")
+        job = interleave_w2(e, tail[:, J * H:J * H + J * N], grp[:, H:])
+        quantise(*job)
+        second_layer(e)
+        yg = turn.tile([P, NB, C], F32, name="yg", align_bytes=64)
+        state["yg", e] = yg
         for b in range(NB):
-            nc.vector.tensor_tensor(yg[:, b, :], state["y", e][:, b, :], gt[:, b, slots(e)], MULT)
-            state["yg", e] = yg
+            nc.vector.tensor_tensor(yg[:, b, :], state["y", e][:, b, :], gt_last[:, b, :], MULT)
+        for b in range(NB):
             scatter(e, b)
             nc.sync.dma_start(out[P * b:P * b + P, :], wins[b][:])

@@ -18,8 +18,8 @@ FP8X4 = mybir.dt.float8_e4m3fn_x4
 MULT = mybir.AluOpType.mult
 SILU = mybir.ActivationFunctionType.Silu
 
-WHOLE = 0
-V_SHARE = ((0, 128, 0, 0, 128, 128), (0, 128, 0, 0, 128, 128), (0, 128, 0, 0, 128, 64), (64, 0, 48, 48, 88, 88))
+V_SHARE = (0, 128, 0, 0, 128, 128)
+V_SHARE_LAST = (0, 0, 128, 64, 48, 64)
 
 FLOPS = 2 * S * (2 * K * H + H * N)
 
@@ -37,12 +37,10 @@ def tile_routed_moe_kernel(tc, xT, w1, w3, w2, gate, offs, out):
 
     with ExitStack() as ctx:
         keep = ctx.enter_context(tc.tile_pool(name="keep", bufs=1))
-        rawp = ctx.enter_context(tc.tile_pool(name="rawp", bufs=5))
-        grpp = ctx.enter_context(tc.tile_pool(name="grpp", bufs=3))
-        grpv = ctx.enter_context(tc.tile_pool(name="grpv", bufs=2))
+        rawp = ctx.enter_context(tc.tile_pool(name="rawp", bufs=8))
+        turn = ctx.enter_context(tc.tile_pool(name="turn", bufs=1))
         wq = ctx.enter_context(tc.tile_pool(name="wq", bufs=2))
         work = ctx.enter_context(tc.tile_pool(name="work", bufs=2))
-        turn = ctx.enter_context(tc.tile_pool(name="turn", bufs=1))
         psum = ctx.enter_context(tc.psum_pool(name="psum", bufs=2))
 
         def quantise(codes, scales, grouped):
@@ -50,7 +48,6 @@ def tile_routed_moe_kernel(tc, xT, w1, w3, w2, gate, offs, out):
 
         lst = keep.tile([P, S // 16], U16, name="lst")
         gt = keep.tile([P, NB, S - C], F32, name="gt")
-        raw2 = keep.tile([P, E - 1, J * N], F32, name="raw2")
         wins = []
         for b in range(NB):
             win = keep.tile([P, T], F32, name=f"win{b}")
@@ -69,83 +66,28 @@ def tile_routed_moe_kernel(tc, xT, w1, w3, w2, gate, offs, out):
             if g == 0:
                 nc.sync.dma_start(lst[:], offs)
             xin = xraw[:].rearrange("p (j c i) -> p c j i", j=J, i=4)
-            xw = keep.tile([P, T], U32, name=f"xw{g}", align_bytes=64)
-            for half in range(2):
-                t0 = half * H
-                cols = slice(t0, t0 + H)
-                if (g, half) in ((0, 0), (2, 0)):
-                    grp = grpv.tile([P, H, J], BF16, name="grp_v", align_bytes=64)
-                    nc.vector.tensor_copy(grp[:].rearrange("p (c i) j -> p c j i", i=4), xin[:, t0 // 4:t0 // 4 + H // 4])
-                else:
-                    grp = grpp.tile([P, H, J], BF16, name="grp_s", align_bytes=64)
-                    nc.scalar.copy(grp[:].rearrange("p (c i) j -> p c j i", i=4), xin[:, t0 // 4:t0 // 4 + H // 4])
-                quantise(xw[:, cols], xs[4 * g:, cols], grp[:])
+            xw = turn.tile([P, T], U32, name=f"x{g + 1}", align_bytes=64)
+            grp_v = turn.tile([P, H, J], BF16, name=f"x{g}", align_bytes=64)
+            grp_s = turn.tile([P, H, J], BF16, name="s", bufs=3, align_bytes=64)
+            nc.vector.tensor_copy(grp_v[:].rearrange("p (c i) j -> p c j i", i=4), xin[:, :H // 4])
+            nc.scalar.copy(grp_s[:].rearrange("p (c i) j -> p c j i", i=4), xin[:, H // 4:])
+            quantise(xw[:, :H], xs[4 * g:, :H], grp_v[:])
+            quantise(xw[:, H:], xs[4 * g:, H:], grp_s[:])
             nc.vector.tensor_copy(gw[:, g, :], xw[:].indirect(lst[:]))
         nc.vector.tensor_copy(gs[:], xs[:].indirect(lst[:]))
+        nc.sync.dma_start(gt[:], gate_rows[:, :, :S - C])
 
-        state = {}
-
-        def slots(e):
-            return slice(C * e, C * e + C)
-
-        def first_layer(e, which, g, tiles):
-            wc, ws = state["w", e, which]
-            if g == 0:
-                state["acc", e, which] = psum.tile([P, 4, C], F32, name=f"acc{which}")
-            acc = state["acc", e, which]
+        def matmuls(acc, wc, ws, e, g, tiles):
             for t in tiles:
                 nc.tensor.matmul_mx(
                     out=acc[:, t, :],
                     lhsT=wc[:, g, P * t:P * t + P].bitcast(FP8X4),
                     lhsT_scale=ws[:, g, P * t:P * t + P],
-                    rhs=gw[:, g, slots(e)].bitcast(FP8X4),
-                    rhs_scale=gs[4 * g:, slots(e)],
+                    rhs=gw[:, g, C * e:C * e + C].bitcast(FP8X4),
+                    rhs_scale=gs[4 * g:, C * e:C * e + C],
                     start=(g == 0 and t == 0),
                     stop=(g == G - 1 and t == 3),
                 )
-
-        def silu(e):
-            sil = turn.tile([P, 4, C], F32, name="sil", align_bytes=64)
-            nc.scalar.activation(sil[:], state["acc", e, 0][:], SILU)
-            state["sil", e] = sil
-
-        def product(e):
-            hb = turn.tile([P, C, 4], BF16, name="odd" if e == E - 2 else "hb", align_bytes=64)
-            nc.vector.tensor_tensor(hb[:], state["sil", e][:].rearrange("p t c -> p c t"), state["acc", e, 1][:].rearrange("p t c -> p c t"), MULT)
-            state["hb", e] = hb
-
-        def second_layer(e):
-            hc = work.tile([P, C], U32, name="hc", align_bytes=64)
-            hs = work.tile([P, C], U8, name="hs", align_bytes=64)
-            quantise(hc[:], hs[:], state["hb", e][:])
-            vc, vs = state["w2", e]
-            y = psum.tile([P, NB, C], F32, name="y")
-            for b in range(NB):
-                nc.tensor.matmul_mx(
-                    out=y[:, b, :],
-                    lhsT=vc[:, P * b:P * b + P].bitcast(FP8X4),
-                    lhsT_scale=vs[:, P * b:P * b + P],
-                    rhs=hc[:].bitcast(FP8X4),
-                    rhs_scale=hs[:],
-                    start=True,
-                    stop=True,
-                )
-            state["y", e] = y
-
-        def gated(e):
-            yg = turn.tile([P, NB, C], F32, name="even" if e == E - 2 else "yg", align_bytes=64)
-            nc.vector.tensor_tensor(yg[:], state["y", e][:], gt[:, :, slots(e)], MULT)
-            state["yg", e] = yg
-
-        def scatter(e, b):
-            nc.vector.tensor_copy(wins[b][:].indirect(lst[:, 8 * e:8 * e + 8]), state["yg", e][:, b, :])
-
-        def interleave_w2(e, raw, grp):
-            nc.scalar.copy(grp.rearrange("p (c i) j -> p c j i", i=4), raw.rearrange("p (j c i) -> p c j i", j=J, i=4))
-            vc = turn.tile([P, N], U32, name="sil", align_bytes=64) if e == E - 1 else work.tile([P, N], U32, name="vc", align_bytes=64)
-            vs = work.tile([P, N], U8, name="vs", align_bytes=64)
-            state["w2", e] = (vc, vs)
-            return (vc[:], vs[:], grp)
 
         def interleave(grp, raw, m, js):
             src = raw.rearrange("p (j m t) -> p m j t", j=J, t=4)
@@ -155,81 +97,97 @@ def tile_routed_moe_kernel(tc, xT, w1, w3, w2, gate, offs, out):
             if m < P:
                 nc.scalar.copy(dst[:, m:, js, :], src[:, m:, js, :])
 
-        items = []
-        for e in range(E):
-            items.extend([(e, which, g) for which in range(2) for g in range(G)])
-            items.append((e, 2, 0))
-        later = []
-        pending = None
-        for step, (e, which, g) in enumerate(items[:-2]):
-            if which == 2:
-                if e == 0:
-                    nc.sync.dma_start(raw2[:], w2_rows[:, :E - 1])
-                    nc.sync.dma_start(gt[:], gate_rows[:, :, :S - C])
-                grp = work.tile([P, N, J], BF16, name="grp2", align_bytes=64)
-                job = interleave_w2(e, raw2[:, e], grp[:])
-            else:
-                if g == 0:
-                    raw = rawp.tile([P, G, J * H], F32, name="raw")
-                    wc = wq.tile([P, G, H], U32, name=f"wc{which}", align_bytes=64)
-                    ws = wq.tile([P, G, H], U8, name=f"ws{which}", align_bytes=64)
-                    state["w", e, which] = (wc, ws)
-                if 2 * e + which >= WHOLE:
-                    nc.sync.dma_start(raw[:, g], w_rows[which][e, :, g])
-                elif g == 0:
-                    nc.sync.dma_start(raw[:], w_rows[which][e])
-                m = V_SHARE[e][G * which + g]
-                if e == E - 1 and G * which + g > 0:
-                    grp = turn.tile([P, H, J], BF16, name="odd" if (G * which + g) % 2 else "even", align_bytes=64)
-                elif m:
-                    grp = grpv.tile([P, H, J], BF16, name="grp_v", align_bytes=64)
-                else:
-                    grp = grpp.tile([P, H, J], BF16, name="grp_s", align_bytes=64)
-                interleave(grp[:], raw[:, g], m, slice(0, J))
-                job = (wc[:, g], ws[:, g], grp[:])
-            if pending:
-                quantise(*pending)
-            pending = job
-            for due, function, args in later:
-                if due == step:
-                    function(*args)
-            if which < 2:
-                later.append((step + 1, first_layer, (e, which, g, range(4))))
-            if which == 0 and g == G - 1:
-                later.append((step + 2, silu, (e,)))
-            if which == 1 and g == G - 1:
-                later.append((step + 2, product, (e,)))
-                later.append((step + 2, second_layer, (e,)))
-                later.append((step + 3, gated, (e,)))
-                later.append((step + 3, scatter, (e, 0)))
-                later.append((step + 3, scatter, (e, 1)))
+        def way_back(e, y, gates, pieces):
+            yg = turn.tile([P, NB, C], F32, name="first", align_bytes=64)
+            for q in range(pieces):
+                part = slice(q * NB // pieces, (q + 1) * NB // pieces)
+                nc.vector.tensor_tensor(yg[:, part, :], y[q][:], gates[:, part, :], MULT)
+            for b in range(NB):
+                nc.vector.tensor_copy(wins[b][:].indirect(lst[:, 8 * e:8 * e + 8]), yg[:, b, :])
 
-        e, g = E - 1, G - 1
-        tail = rawp.tile([P, J * H + J * N + NB * C], F32, name="raw")
-        half = J * H // 2
-        for q in range(2):
-            nc.sync.dma_start(tail[:, q * half:q * half + half], w_rows[1][e, :, g, q * half:q * half + half])
-        nc.sync.dma_start(tail[:, J * H:J * H + J * N], w2_rows[:, e])
-        gt_last = tail[:, J * H + J * N:].rearrange("p (b s) -> p b s", b=NB)
-        nc.sync.dma_start(gt_last, gate_rows[:, :, S - C:])
-        quantise(*pending)
-        first_layer(e, 1, g - 1, range(4))
-        grp = turn.tile([P, H + N, J], BF16, name="even", align_bytes=64)
-        m = V_SHARE[e][-1]
-        interleave(grp[:, :H], tail[:, :J * H], m, slice(0, 2))
-        interleave(grp[:, :H], tail[:, :J * H], m, slice(2, 4))
-        for u in range(2):
-            cols = slice(u * H // 2, (u + 1) * H // 2)
-            quantise(wc[:, g, cols], ws[:, g, cols], grp[:, cols, :])
-            first_layer(e, 1, g, range(2 * u, 2 * u + 2))
-        product(e)
-        job = interleave_w2(e, tail[:, J * H:J * H + J * N], grp[:, H:])
-        quantise(*job)
-        second_layer(e)
-        yg = turn.tile([P, NB, C], F32, name="yg", align_bytes=64)
-        state["yg", e] = yg
+        for e in range(E):
+            last = e == E - 1
+            share = V_SHARE_LAST if last else V_SHARE
+            accs = [psum.tile([P, 4, C], F32, name=f"acc{which}") for which in range(2)]
+            codes = [wq.tile([P, G, H], U32, name=f"wc{which}", align_bytes=64) for which in range(2)]
+            scales = [wq.tile([P, G, H], U8, name=f"ws{which}", align_bytes=64) for which in range(2)]
+
+            def finish(which, g, grp):
+                quantise(codes[which][:, g], scales[which][:, g], grp)
+                matmuls(accs[which], codes[which], scales[which], e, g, range(4))
+
+            pending = None
+            for i in range(2 * G - 1):
+                which, g = divmod(i, G)
+                raw = rawp.tile([P, J * H], F32, name="raw")
+                nc.sync.dma_start(raw[:], w_rows[which][e, :, g])
+                if i == 0:
+                    grp = turn.tile([P, H, J], BF16, name="first", align_bytes=64)
+                elif share[i]:
+                    grp = turn.tile([P, H, J], BF16, name="v", bufs=2, align_bytes=64)
+                else:
+                    grp = turn.tile([P, H, J], BF16, name="s", bufs=3, align_bytes=64)
+                interleave(grp[:], raw[:], share[i], slice(0, J))
+                if pending:
+                    finish(*pending)
+                pending = (which, g, grp[:])
+                if i == 1 and e > 0:
+                    way_back(e - 1, y, gates, 1)
+
+            g = G - 1
+            tail = rawp.tile([P, J * H + J * N + NB * C], F32, name="raw")
+            pieces = 2 if last else 1
+            width = J * H // pieces
+            for q in range(pieces):
+                nc.sync.dma_start(tail[:, q * width:q * width + width], w_rows[1][e, :, g, q * width:q * width + width])
+            nc.sync.dma_start(tail[:, J * H:J * H + J * N], w2_rows[:, e])
+            if last:
+                gates = tail[:, J * H + J * N:].rearrange("p (b s) -> p b s", b=NB)
+                nc.sync.dma_start(gates, gate_rows[:, :, S - C:])
+            else:
+                gates = gt[:, :, C * e:C * e + C]
+            grp = turn.tile([P, H + N, J], BF16, name="v", bufs=2, align_bytes=64)
+            interleave(grp[:, :H], tail[:, :J * H], share[-1], slice(0, J // pieces))
+            finish(*pending)
+            if last:
+                src = tail[:, :J * H].rearrange("p (j m t) -> p m j t", j=J, t=4)
+                dst = grp[:, :H].rearrange("p (t m) j -> p m j t", t=4)
+                for u in range(2):
+                    nc.vector.tensor_copy(dst[:, :, 2:, 2 * u:2 * u + 2], src[:, :, 2:, 2 * u:2 * u + 2])
+            if last:
+                sil = turn.tile([P, 4, C], F32, name="v", bufs=2, align_bytes=64)
+                hc = turn.tile([P, C], U32, name="v", bufs=2, align_bytes=64)
+            else:
+                sil = work.tile([P, 4, C], F32, name="sil")
+                hc = work.tile([P, C], U32, name="hc", align_bytes=64)
+            nc.scalar.activation(sil[:], accs[0][:], SILU)
+            nc.scalar.copy(grp[:, H:].rearrange("p (c i) j -> p c j i", i=4), tail[:, J * H:J * H + J * N].rearrange("p (j c i) -> p c j i", j=J, i=4))
+            for u in range(pieces):
+                cols = slice(u * H // pieces, (u + 1) * H // pieces)
+                quantise(codes[1][:, g, cols], scales[1][:, g, cols], grp[:, cols, :])
+                matmuls(accs[1], codes[1], scales[1], e, g, range(u * 4 // pieces, (u + 1) * 4 // pieces))
+            vs = work.tile([P, N], U8, name="vs", align_bytes=64)
+            if not last:
+                vc = work.tile([P, N], U32, name="vc", align_bytes=64)
+                quantise(vc[:], vs[:], grp[:, H:])
+            hb = turn.tile([P, C, 4], BF16, name="h", align_bytes=64)
+            nc.vector.tensor_tensor(hb[:], sil[:].rearrange("p t c -> p c t"), accs[1][:].rearrange("p t c -> p c t"), MULT)
+            if last:
+                vc = turn.tile([P, N], U32, name="v", bufs=2, align_bytes=64)
+                quantise(vc[:], vs[:], grp[:, H:])
+            hs = work.tile([P, C], U8, name="hs", align_bytes=64)
+            quantise(hc[:], hs[:], hb[:])
+            y = [psum.tile([P, NB // pieces, C], F32, name="y") for q in range(pieces)]
+            for b in range(NB):
+                nc.tensor.matmul_mx(
+                    out=y[b * pieces // NB][:, b % (NB // pieces), :],
+                    lhsT=vc[:, P * b:P * b + P].bitcast(FP8X4),
+                    lhsT_scale=vs[:, P * b:P * b + P],
+                    rhs=hc[:].bitcast(FP8X4),
+                    rhs_scale=hs[:],
+                    start=True,
+                    stop=True,
+                )
+        way_back(E - 1, y, gates, NB)
         for b in range(NB):
-            nc.vector.tensor_tensor(yg[:, b, :], state["y", e][:, b, :], gt_last[:, b, :], MULT)
-        for b in range(NB):
-            scatter(e, b)
             nc.sync.dma_start(out[P * b:P * b + P, :], wins[b][:])

@@ -18,6 +18,7 @@ FP8X4 = mybir.dt.float8_e4m3fn_x4
 MULT = mybir.AluOpType.mult
 SILU = mybir.ActivationFunctionType.Silu
 
+WHOLE = 5
 V_SHARE = (0, 128, 0, 0, 128, 128)
 V_SHARE_LAST = (0, 0, 128, 64, 48, 64)
 
@@ -37,7 +38,7 @@ def tile_routed_moe_kernel(tc, xT, w1, w3, w2, gate, offs, out):
 
     with ExitStack() as ctx:
         keep = ctx.enter_context(tc.tile_pool(name="keep", bufs=1))
-        rawp = ctx.enter_context(tc.tile_pool(name="rawp", bufs=8))
+        rawp = ctx.enter_context(tc.tile_pool(name="rawp", bufs=5))
         turn = ctx.enter_context(tc.tile_pool(name="turn", bufs=1))
         wq = ctx.enter_context(tc.tile_pool(name="wq", bufs=2))
         work = ctx.enter_context(tc.tile_pool(name="work", bufs=2))
@@ -98,7 +99,7 @@ def tile_routed_moe_kernel(tc, xT, w1, w3, w2, gate, offs, out):
                 nc.scalar.copy(dst[:, m:, js, :], src[:, m:, js, :])
 
         def way_back(e, y, gates, pieces):
-            yg = turn.tile([P, NB, C], F32, name="first", align_bytes=64)
+            yg = turn.tile([P, NB, C], F32, name="first" if 2 * e + 2 >= WHOLE else "yg", align_bytes=64)
             for q in range(pieces):
                 part = slice(q * NB // pieces, (q + 1) * NB // pieces)
                 nc.vector.tensor_tensor(yg[:, part, :], y[q][:], gates[:, part, :], MULT)
@@ -119,15 +120,19 @@ def tile_routed_moe_kernel(tc, xT, w1, w3, w2, gate, offs, out):
             pending = None
             for i in range(2 * G - 1):
                 which, g = divmod(i, G)
-                raw = rawp.tile([P, J * H], F32, name="raw")
-                nc.sync.dma_start(raw[:], w_rows[which][e, :, g])
+                if g == 0:
+                    raw = rawp.tile([P, G, J * H], F32, name="raw")
+                if 2 * e + which >= WHOLE:
+                    nc.sync.dma_start(raw[:, g], w_rows[which][e, :, g])
+                elif g == 0:
+                    nc.sync.dma_start(raw[:], w_rows[which][e])
                 if i == 0:
                     grp = turn.tile([P, H, J], BF16, name="first", align_bytes=64)
                 elif share[i]:
                     grp = turn.tile([P, H, J], BF16, name="v", bufs=2, align_bytes=64)
                 else:
                     grp = turn.tile([P, H, J], BF16, name="s", bufs=3, align_bytes=64)
-                interleave(grp[:], raw[:], share[i], slice(0, J))
+                interleave(grp[:], raw[:, g], share[i], slice(0, J))
                 if pending:
                     finish(*pending)
                 pending = (which, g, grp[:])
@@ -138,7 +143,8 @@ def tile_routed_moe_kernel(tc, xT, w1, w3, w2, gate, offs, out):
             tail = rawp.tile([P, J * H + J * N + NB * C], F32, name="raw")
             pieces = 2 if last else 1
             width = J * H // pieces
-            for q in range(pieces):
+            chunk = raw[:, g] if 2 * e + 1 < WHOLE else tail[:, :J * H]
+            for q in range(pieces if 2 * e + 1 >= WHOLE else 0):
                 nc.sync.dma_start(tail[:, q * width:q * width + width], w_rows[1][e, :, g, q * width:q * width + width])
             nc.sync.dma_start(tail[:, J * H:J * H + J * N], w2_rows[:, e])
             if last:
@@ -147,7 +153,7 @@ def tile_routed_moe_kernel(tc, xT, w1, w3, w2, gate, offs, out):
             else:
                 gates = gt[:, :, C * e:C * e + C]
             grp = turn.tile([P, H + N, J], BF16, name="v", bufs=2, align_bytes=64)
-            interleave(grp[:, :H], tail[:, :J * H], share[-1], slice(0, J // pieces))
+            interleave(grp[:, :H], chunk, share[-1], slice(0, J // pieces))
             finish(*pending)
             if last:
                 src = tail[:, :J * H].rearrange("p (j m t) -> p m j t", j=J, t=4)

@@ -19,8 +19,8 @@ MULT = mybir.AluOpType.mult
 SILU = mybir.ActivationFunctionType.Silu
 
 WHOLE = 5
-V_SHARE = (0, 128, 0, 0, 128, 128)
-V_SHARE_LAST = (0, 0, 128, 64, 48, 64)
+V_SHARE = (0, 128, 0, 0, 64, 128)
+V_SHARE_LAST = (0, 0, 128, 64, 64, 64)
 
 FLOPS = 2 * S * (2 * K * H + H * N)
 
@@ -90,13 +90,13 @@ def tile_routed_moe_kernel(tc, xT, w1, w3, w2, gate, offs, out):
                     stop=(g == G - 1 and t == 3),
                 )
 
-        def interleave(grp, raw, m, js):
+        def interleave(grp, raw, m, ts):
             src = raw.rearrange("p (j m t) -> p m j t", j=J, t=4)
             dst = grp.rearrange("p (t m) j -> p m j t", t=4)
             if m:
-                nc.vector.tensor_copy(dst[:, :m, js, :], src[:, :m, js, :])
+                nc.vector.tensor_copy(dst[:, :m, :, ts], src[:, :m, :, ts])
             if m < P:
-                nc.scalar.copy(dst[:, m:, js, :], src[:, m:, js, :])
+                nc.scalar.copy(dst[:, m:, :, ts], src[:, m:, :, ts])
 
         def way_back(e, y, gates, pieces):
             yg = turn.tile([P, NB, C], F32, name="first" if 2 * e + 2 >= WHOLE else "yg", align_bytes=64)
@@ -142,10 +142,9 @@ def tile_routed_moe_kernel(tc, xT, w1, w3, w2, gate, offs, out):
             g = G - 1
             tail = rawp.tile([P, J * H + J * N + NB * C], F32, name="raw")
             pieces = 2 if last else 1
-            width = J * H // pieces
             chunk = raw[:, g] if 2 * e + 1 < WHOLE else tail[:, :J * H]
-            for q in range(pieces if 2 * e + 1 >= WHOLE else 0):
-                nc.sync.dma_start(tail[:, q * width:q * width + width], w_rows[1][e, :, g, q * width:q * width + width])
+            if 2 * e + 1 >= WHOLE:
+                nc.sync.dma_start(chunk, w_rows[1][e, :, g])
             nc.sync.dma_start(tail[:, J * H:J * H + J * N], w2_rows[:, e])
             if last:
                 gates = tail[:, J * H + J * N:].rearrange("p (b s) -> p b s", b=NB)
@@ -153,20 +152,20 @@ def tile_routed_moe_kernel(tc, xT, w1, w3, w2, gate, offs, out):
             else:
                 gates = gt[:, :, C * e:C * e + C]
             grp = turn.tile([P, H + N, J], BF16, name="v", bufs=2, align_bytes=64)
-            interleave(grp[:, :H], chunk, share[-1], slice(0, J // pieces))
-            finish(*pending)
             if last:
-                src = tail[:, :J * H].rearrange("p (j m t) -> p m j t", j=J, t=4)
-                dst = grp[:, :H].rearrange("p (t m) j -> p m j t", t=4)
-                for u in range(2):
-                    nc.vector.tensor_copy(dst[:, :, 2:, 2 * u:2 * u + 2], src[:, :, 2:, 2 * u:2 * u + 2])
+                finish(*pending)
+                interleave(grp[:, :H], chunk, P, slice(0, 2))
+                interleave(grp[:, :H], chunk, share[-1], slice(2, 4))
+            else:
+                interleave(grp[:, :H], chunk, share[-1], slice(0, 4))
+                finish(*pending)
             if last:
-                sil = turn.tile([P, 4, C], F32, name="v", bufs=2, align_bytes=64)
+                sil = turn.tile([P, C, 4], F32, name="v", bufs=2, align_bytes=64)
                 hc = turn.tile([P, C], U32, name="v", bufs=2, align_bytes=64)
             else:
-                sil = work.tile([P, 4, C], F32, name="sil")
+                sil = work.tile([P, C, 4], F32, name="sil")
                 hc = work.tile([P, C], U32, name="hc", align_bytes=64)
-            nc.scalar.activation(sil[:], accs[0][:], SILU)
+            nc.scalar.activation(sil[:], accs[0][:].rearrange("p t c -> p c t"), SILU)
             nc.scalar.copy(grp[:, H:].rearrange("p (c i) j -> p c j i", i=4), tail[:, J * H:J * H + J * N].rearrange("p (j c i) -> p c j i", j=J, i=4))
             for u in range(pieces):
                 cols = slice(u * H // pieces, (u + 1) * H // pieces)
@@ -177,7 +176,7 @@ def tile_routed_moe_kernel(tc, xT, w1, w3, w2, gate, offs, out):
                 vc = work.tile([P, N], U32, name="vc", align_bytes=64)
                 quantise(vc[:], vs[:], grp[:, H:])
             hb = turn.tile([P, C, 4], BF16, name="h", align_bytes=64)
-            nc.vector.tensor_tensor(hb[:], sil[:].rearrange("p t c -> p c t"), accs[1][:].rearrange("p t c -> p c t"), MULT)
+            nc.vector.tensor_tensor(hb[:], sil[:], accs[1][:].rearrange("p t c -> p c t"), MULT)
             if last:
                 vc = turn.tile([P, N], U32, name="v", bufs=2, align_bytes=64)
                 quantise(vc[:], vs[:], grp[:, H:])

@@ -20,7 +20,7 @@ SILU = mybir.ActivationFunctionType.Silu
 
 WHOLE = 5
 V_SHARE = (0, 128, 0, 0, 64, 128)
-V_SHARE_LAST = (0, 0, 128, 64, 64, 64)
+V_SHARE_LAST = (0, 0, 128, 64, 48, 64)
 
 FLOPS = 2 * S * (2 * K * H + H * N)
 
@@ -144,7 +144,9 @@ def tile_routed_moe_kernel(tc, xT, w1, w3, w2, gate, offs, out):
             pieces = 2 if last else 1
             chunk = raw[:, g] if 2 * e + 1 < WHOLE else tail[:, :J * H]
             if 2 * e + 1 >= WHOLE:
-                nc.sync.dma_start(chunk, w_rows[1][e, :, g])
+                width = J * H // pieces
+                for q in range(pieces):
+                    nc.sync.dma_start(chunk[:, q * width:q * width + width], w_rows[1][e, :, g, q * width:q * width + width])
             nc.sync.dma_start(tail[:, J * H:J * H + J * N], w2_rows[:, e])
             if last:
                 gates = tail[:, J * H + J * N:].rearrange("p (b s) -> p b s", b=NB)
@@ -153,9 +155,14 @@ def tile_routed_moe_kernel(tc, xT, w1, w3, w2, gate, offs, out):
                 gates = gt[:, :, C * e:C * e + C]
             grp = turn.tile([P, H + N, J], BF16, name="v", bufs=2, align_bytes=64)
             if last:
+                src = chunk.rearrange("p (j m t) -> p m t j", j=J, t=4)
+                dst = grp[:, :H].rearrange("p (t m) j -> p m t j", t=4)
+                m = share[-1]
+                nc.vector.tensor_copy(dst[:, :m, :, :2], src[:, :m, :, :2])
+                nc.scalar.copy(dst[:, m:, :, :2], src[:, m:, :, :2])
                 finish(*pending)
-                interleave(grp[:, :H], chunk, P, slice(0, 2))
-                interleave(grp[:, :H], chunk, share[-1], slice(2, 4))
+                for u in range(2):
+                    nc.vector.tensor_copy(dst[:, :, 2 * u:2 * u + 2, 2:], src[:, :, 2 * u:2 * u + 2, 2:])
             else:
                 interleave(grp[:, :H], chunk, share[-1], slice(0, 4))
                 finish(*pending)
@@ -166,27 +173,30 @@ def tile_routed_moe_kernel(tc, xT, w1, w3, w2, gate, offs, out):
                 sil = work.tile([P, C, 4], F32, name="sil")
                 hc = work.tile([P, C], U32, name="hc", align_bytes=64)
             nc.scalar.activation(sil[:], accs[0][:].rearrange("p t c -> p c t"), SILU)
-            nc.scalar.copy(grp[:, H:].rearrange("p (c i) j -> p c j i", i=4), tail[:, J * H:J * H + J * N].rearrange("p (j c i) -> p c j i", j=J, i=4))
+            for q in range(pieces):
+                part = slice(q * N // 4 // pieces, (q + 1) * N // 4 // pieces)
+                nc.scalar.copy(grp[:, H:].rearrange("p (c i) j -> p c j i", i=4)[:, part], tail[:, J * H:J * H + J * N].rearrange("p (j c i) -> p c j i", j=J, i=4)[:, part])
             for u in range(pieces):
                 cols = slice(u * H // pieces, (u + 1) * H // pieces)
                 quantise(codes[1][:, g, cols], scales[1][:, g, cols], grp[:, cols, :])
                 matmuls(accs[1], codes[1], scales[1], e, g, range(u * 4 // pieces, (u + 1) * 4 // pieces))
             vs = work.tile([P, N], U8, name="vs", align_bytes=64)
-            if not last:
-                vc = work.tile([P, N], U32, name="vc", align_bytes=64)
-                quantise(vc[:], vs[:], grp[:, H:])
+            vc = work.tile([P, N], U32, name="vc", align_bytes=64)
+            blocks = [vc[:, :P], vc[:, P:]]
+            quantise(vc[:, :N // pieces], vs[:, :N // pieces], grp[:, H:H + N // pieces])
             hb = turn.tile([P, C, 4], BF16, name="h", align_bytes=64)
             nc.vector.tensor_tensor(hb[:], sil[:], accs[1][:].rearrange("p t c -> p c t"), MULT)
             if last:
-                vc = turn.tile([P, N], U32, name="v", bufs=2, align_bytes=64)
-                quantise(vc[:], vs[:], grp[:, H:])
+                vc = turn.tile([P, P], U32, name="v", bufs=2, align_bytes=64)
+                blocks[1] = vc[:]
+                quantise(vc[:], vs[:, P:], grp[:, H + P:])
             hs = work.tile([P, C], U8, name="hs", align_bytes=64)
             quantise(hc[:], hs[:], hb[:])
             y = [psum.tile([P, NB // pieces, C], F32, name="y") for q in range(pieces)]
             for b in range(NB):
                 nc.tensor.matmul_mx(
                     out=y[b * pieces // NB][:, b % (NB // pieces), :],
-                    lhsT=vc[:, P * b:P * b + P].bitcast(FP8X4),
+                    lhsT=blocks[b].bitcast(FP8X4),
                     lhsT_scale=vs[:, P * b:P * b + P],
                     rhs=hc[:].bitcast(FP8X4),
                     rhs_scale=hs[:],

@@ -8,6 +8,8 @@ P = 128
 J = 4
 G = K // (P * J)
 NB = N // P
+TILES = H // P
+LINE = 4
 
 F32 = mybir.dt.float32
 BF16 = mybir.dt.bfloat16
@@ -25,10 +27,6 @@ V_SHARE_LAST = (0, 0, 128, 64, 48, 64)
 FLOPS = 2 * S * (2 * K * H + H * N)
 
 
-def flat(grouped):
-    return grouped.rearrange("p w j -> p (w j)")
-
-
 def tile_routed_moe_kernel(tc, xT, w1, w3, w2, gate, offs, out):
     nc = tc.nc
     x_rows = xT.rearrange("(g p j) n -> g p (j n)", p=P, j=J)
@@ -44,78 +42,86 @@ def tile_routed_moe_kernel(tc, xT, w1, w3, w2, gate, offs, out):
         work = ctx.enter_context(tc.tile_pool(name="work", bufs=2))
         psum = ctx.enter_context(tc.psum_pool(name="psum", bufs=2))
 
-        def quantise(codes, scales, grouped):
-            nc.vector.quantize_mx(out=codes.bitcast(FP8X4), scales=scales, in_=flat(grouped))
+        def quantise(words, scales, grouped):
+            nc.vector.quantize_mx(out=words.bitcast(FP8X4), scales=scales, in_=grouped.rearrange("p c j -> p (c j)"))
+
+        def vector_ring(shape, dtype):
+            return turn.tile(shape, dtype, name="vector_ring", bufs=2, align_bytes=64)
+
+        def scalar_ring():
+            return turn.tile([P, H, J], BF16, name="scalar_ring", bufs=3, align_bytes=64)
+
+        def by_lines(raw, grouped):
+            return raw.rearrange("p (j c i) -> p c j i", j=J, i=LINE), grouped.rearrange("p (c i) j -> p c j i", i=LINE)
 
         lst = keep.tile([P, S // 16], U16, name="lst")
-        gt = keep.tile([P, NB, S - C], F32, name="gt")
+        gates_early = keep.tile([P, NB, S - C], F32, name="gates_early")
         wins = []
         for b in range(NB):
             win = keep.tile([P, T], F32, name=f"win{b}")
             nc.vector.memset(win[:], 0.0)
             wins.append(win)
-        warm = keep.tile([P, 1], F32, name="warm")
-        nc.vector.memset(warm[:], 0.0)
-        nc.scalar.activation(warm[:], warm[:], SILU)
 
-        gw = keep.tile([P, G, S], U32, name="gw", align_bytes=64)
-        gs = keep.tile([P, S], U8, name="gs", align_bytes=64)
-        xs = keep.tile([P, T], U8, name="xs", align_bytes=64)
+        slot_words = keep.tile([P, G, S], U32, name="slot_words", align_bytes=64)
+        slot_scales = keep.tile([P, S], U8, name="slot_scales", align_bytes=64)
+        token_scales = keep.tile([P, T], U8, name="token_scales", align_bytes=64)
+        half = T // 2
         for g in range(G):
             xraw = rawp.tile([P, J * T], F32, name="raw")
             nc.sync.dma_start(xraw[:], x_rows[g])
             if g == 0:
                 nc.sync.dma_start(lst[:], offs)
-            xin = xraw[:].rearrange("p (j c i) -> p c j i", j=J, i=4)
-            xw = turn.tile([P, T], U32, name=f"x{g + 1}", align_bytes=64)
-            grp_v = turn.tile([P, H, J], BF16, name=f"x{g}", align_bytes=64)
-            grp_s = turn.tile([P, H, J], BF16, name="s", bufs=3, align_bytes=64)
-            nc.vector.tensor_copy(grp_v[:].rearrange("p (c i) j -> p c j i", i=4), xin[:, :H // 4])
-            nc.scalar.copy(grp_s[:].rearrange("p (c i) j -> p c j i", i=4), xin[:, H // 4:])
-            quantise(xw[:, :H], xs[4 * g:, :H], grp_v[:])
-            quantise(xw[:, H:], xs[4 * g:, H:], grp_s[:])
-            nc.vector.tensor_copy(gw[:, g, :], xw[:].indirect(lst[:]))
-        nc.vector.tensor_copy(gs[:], xs[:].indirect(lst[:]))
-        nc.sync.dma_start(gt[:], gate_rows[:, :, :S - C])
+            token_words = turn.tile([P, T], U32, name=f"x{g + 1}", align_bytes=64)
+            grouped = [turn.tile([P, half, J], BF16, name=f"x{g}", align_bytes=64), scalar_ring()]
+            for u, copy in enumerate((nc.vector.tensor_copy, nc.scalar.copy)):
+                src = xraw[:].rearrange("p (j c i) -> p c j i", j=J, i=LINE)[:, u * half // LINE:(u + 1) * half // LINE]
+                copy(grouped[u][:].rearrange("p (c i) j -> p c j i", i=LINE), src)
+            for u in range(2):
+                tokens = slice(u * half, (u + 1) * half)
+                quantise(token_words[:, tokens], token_scales[4 * g:, tokens], grouped[u][:])
+            nc.vector.tensor_copy(slot_words[:, g, :], token_words[:].indirect(lst[:]))
+        nc.vector.tensor_copy(slot_scales[:], token_scales[:].indirect(lst[:]))
+        nc.sync.dma_start(gates_early[:], gate_rows[:, :, :S - C])
 
-        def matmuls(acc, wc, ws, e, g, tiles):
+        def first_layer(acc, words, scales, e, g, tiles):
             for t in tiles:
                 nc.tensor.matmul_mx(
                     out=acc[:, t, :],
-                    lhsT=wc[:, g, P * t:P * t + P].bitcast(FP8X4),
-                    lhsT_scale=ws[:, g, P * t:P * t + P],
-                    rhs=gw[:, g, C * e:C * e + C].bitcast(FP8X4),
-                    rhs_scale=gs[4 * g:, C * e:C * e + C],
+                    lhsT=words[:, g, P * t:P * t + P].bitcast(FP8X4),
+                    lhsT_scale=scales[:, g, P * t:P * t + P],
+                    rhs=slot_words[:, g, C * e:C * e + C].bitcast(FP8X4),
+                    rhs_scale=slot_scales[4 * g:, C * e:C * e + C],
                     start=(g == 0 and t == 0),
-                    stop=(g == G - 1 and t == 3),
+                    stop=(g == G - 1 and t == TILES - 1),
                 )
 
-        def interleave(grp, raw, m, ts):
-            src = raw.rearrange("p (j m t) -> p m j t", j=J, t=4)
-            dst = grp.rearrange("p (t m) j -> p m j t", t=4)
+        def interleave(grouped, raw, m):
+            src = raw.rearrange("p (j m t) -> p m j t", j=J, t=TILES)
+            dst = grouped.rearrange("p (t m) j -> p m j t", t=TILES)
             if m:
-                nc.vector.tensor_copy(dst[:, :m, :, ts], src[:, :m, :, ts])
+                nc.vector.tensor_copy(dst[:, :m], src[:, :m])
             if m < P:
-                nc.scalar.copy(dst[:, m:, :, ts], src[:, m:, :, ts])
+                nc.scalar.copy(dst[:, m:], src[:, m:])
 
-        def way_back(e, y, gates, pieces):
-            yg = turn.tile([P, NB, C], F32, name="first" if 2 * e + 2 >= WHOLE else "yg", align_bytes=64)
-            for q in range(pieces):
-                part = slice(q * NB // pieces, (q + 1) * NB // pieces)
-                nc.vector.tensor_tensor(yg[:, part, :], y[q][:], gates[:, part, :], MULT)
+        def way_back(e, banks, gates):
+            gated = turn.tile([P, NB, C], F32, name="first" if 2 * (e + 1) >= WHOLE else "gated", align_bytes=64)
+            width = NB // len(banks)
+            for q, bank in enumerate(banks):
+                blocks = slice(q * width, (q + 1) * width)
+                nc.vector.tensor_tensor(gated[:, blocks, :], bank[:], gates[:, blocks, :], MULT)
             for b in range(NB):
-                nc.vector.tensor_copy(wins[b][:].indirect(lst[:, 8 * e:8 * e + 8]), yg[:, b, :])
+                nc.vector.tensor_copy(wins[b][:].indirect(lst[:, e * C // 16:(e + 1) * C // 16]), gated[:, b, :])
 
         for e in range(E):
             last = e == E - 1
             share = V_SHARE_LAST if last else V_SHARE
-            accs = [psum.tile([P, 4, C], F32, name=f"acc{which}") for which in range(2)]
-            codes = [wq.tile([P, G, H], U32, name=f"wc{which}", align_bytes=64) for which in range(2)]
-            scales = [wq.tile([P, G, H], U8, name=f"ws{which}", align_bytes=64) for which in range(2)]
+            accs = [psum.tile([P, TILES, C], F32, name=f"acc{which}") for which in range(2)]
+            words = [wq.tile([P, G, H], U32, name=f"words{which}", align_bytes=64) for which in range(2)]
+            scales = [wq.tile([P, G, H], U8, name=f"scales{which}", align_bytes=64) for which in range(2)]
 
-            def finish(which, g, grp):
-                quantise(codes[which][:, g], scales[which][:, g], grp)
-                matmuls(accs[which], codes[which], scales[which], e, g, range(4))
+            def finish(which, g, grouped):
+                quantise(words[which][:, g], scales[which][:, g], grouped)
+                first_layer(accs[which], words[which], scales[which], e, g, range(TILES))
 
             pending = None
             for i in range(2 * G - 1):
@@ -127,82 +133,84 @@ def tile_routed_moe_kernel(tc, xT, w1, w3, w2, gate, offs, out):
                 elif g == 0:
                     nc.sync.dma_start(raw[:], w_rows[which][e])
                 if i == 0:
-                    grp = turn.tile([P, H, J], BF16, name="first", align_bytes=64)
+                    grouped = turn.tile([P, H, J], BF16, name="first", align_bytes=64)
                 elif share[i]:
-                    grp = turn.tile([P, H, J], BF16, name="v", bufs=2, align_bytes=64)
+                    grouped = vector_ring([P, H, J], BF16)
                 else:
-                    grp = turn.tile([P, H, J], BF16, name="s", bufs=3, align_bytes=64)
-                interleave(grp[:], raw[:, g], share[i], slice(0, J))
+                    grouped = scalar_ring()
+                interleave(grouped[:], raw[:, g], share[i])
                 if pending:
                     finish(*pending)
-                pending = (which, g, grp[:])
+                pending = (which, g, grouped[:])
                 if i == 1 and e > 0:
-                    way_back(e - 1, y, gates, 1)
+                    way_back(e - 1, banks, gates)
 
             g = G - 1
+            parts = 2 if last else 1
             tail = rawp.tile([P, J * H + J * N + NB * C], F32, name="raw")
-            pieces = 2 if last else 1
-            chunk = raw[:, g] if 2 * e + 1 < WHOLE else tail[:, :J * H]
             if 2 * e + 1 >= WHOLE:
-                width = J * H // pieces
-                for q in range(pieces):
-                    nc.sync.dma_start(chunk[:, q * width:q * width + width], w_rows[1][e, :, g, q * width:q * width + width])
-            nc.sync.dma_start(tail[:, J * H:J * H + J * N], w2_rows[:, e])
+                chunk = tail[:, :J * H]
+                width = J * H // parts
+                for q in range(parts):
+                    nc.sync.dma_start(chunk[:, q * width:(q + 1) * width], w_rows[1][e, :, g, q * width:(q + 1) * width])
+            else:
+                chunk = raw[:, g]
+            raw2 = tail[:, J * H:J * H + J * N]
+            nc.sync.dma_start(raw2, w2_rows[:, e])
             if last:
                 gates = tail[:, J * H + J * N:].rearrange("p (b s) -> p b s", b=NB)
                 nc.sync.dma_start(gates, gate_rows[:, :, S - C:])
             else:
-                gates = gt[:, :, C * e:C * e + C]
-            grp = turn.tile([P, H + N, J], BF16, name="v", bufs=2, align_bytes=64)
+                gates = gates_early[:, :, C * e:C * e + C]
+            grouped = vector_ring([P, H + N, J], BF16)
             if last:
-                src = chunk.rearrange("p (j m t) -> p m t j", j=J, t=4)
-                dst = grp[:, :H].rearrange("p (t m) j -> p m t j", t=4)
+                src = chunk.rearrange("p (j m t) -> p m t j", j=J, t=TILES)
+                dst = grouped[:, :H].rearrange("p (t m) j -> p m t j", t=TILES)
                 m = share[-1]
                 nc.vector.tensor_copy(dst[:, :m, :, :2], src[:, :m, :, :2])
                 nc.scalar.copy(dst[:, m:, :, :2], src[:, m:, :, :2])
                 finish(*pending)
-                for u in range(2):
-                    nc.vector.tensor_copy(dst[:, :, 2 * u:2 * u + 2, 2:], src[:, :, 2 * u:2 * u + 2, 2:])
+                for q in range(parts):
+                    nc.vector.tensor_copy(dst[:, :, 2 * q:2 * q + 2, 2:], src[:, :, 2 * q:2 * q + 2, 2:])
+                sil = vector_ring([P, C, TILES], F32)
+                h_words = vector_ring([P, C], U32)
             else:
-                interleave(grp[:, :H], chunk, share[-1], slice(0, 4))
+                interleave(grouped[:, :H], chunk, share[-1])
                 finish(*pending)
-            if last:
-                sil = turn.tile([P, C, 4], F32, name="v", bufs=2, align_bytes=64)
-                hc = turn.tile([P, C], U32, name="v", bufs=2, align_bytes=64)
-            else:
-                sil = work.tile([P, C, 4], F32, name="sil")
-                hc = work.tile([P, C], U32, name="hc", align_bytes=64)
+                sil = work.tile([P, C, TILES], F32, name="sil")
+                h_words = work.tile([P, C], U32, name="h_words", align_bytes=64)
             nc.scalar.activation(sil[:], accs[0][:].rearrange("p t c -> p c t"), SILU)
-            for q in range(pieces):
-                part = slice(q * N // 4 // pieces, (q + 1) * N // 4 // pieces)
-                nc.scalar.copy(grp[:, H:].rearrange("p (c i) j -> p c j i", i=4)[:, part], tail[:, J * H:J * H + J * N].rearrange("p (j c i) -> p c j i", j=J, i=4)[:, part])
-            for u in range(pieces):
-                cols = slice(u * H // pieces, (u + 1) * H // pieces)
-                quantise(codes[1][:, g, cols], scales[1][:, g, cols], grp[:, cols, :])
-                matmuls(accs[1], codes[1], scales[1], e, g, range(u * 4 // pieces, (u + 1) * 4 // pieces))
-            vs = work.tile([P, N], U8, name="vs", align_bytes=64)
-            vc = work.tile([P, N], U32, name="vc", align_bytes=64)
-            blocks = [vc[:, :P], vc[:, P:]]
-            quantise(vc[:, :N // pieces], vs[:, :N // pieces], grp[:, H:H + N // pieces])
-            hb = turn.tile([P, C, 4], BF16, name="h", align_bytes=64)
-            nc.vector.tensor_tensor(hb[:], sil[:], accs[1][:].rearrange("p t c -> p c t"), MULT)
+            src, dst = by_lines(raw2, grouped[:, H:])
+            width = N // LINE // parts
+            for q in range(parts):
+                nc.scalar.copy(dst[:, q * width:(q + 1) * width], src[:, q * width:(q + 1) * width])
+            for q in range(parts):
+                cols = slice(q * H // parts, (q + 1) * H // parts)
+                quantise(words[1][:, g, cols], scales[1][:, g, cols], grouped[:, cols, :])
+                first_layer(accs[1], words[1], scales[1], e, g, range(q * TILES // parts, (q + 1) * TILES // parts))
+
+            w2_scales = work.tile([P, N], U8, name="w2_scales", align_bytes=64)
+            w2_words = work.tile([P, N], U32, name="w2_words", align_bytes=64)
+            w2_blocks = [w2_words[:, P * b:P * b + P] for b in range(NB)]
+            quantise(w2_words[:, :N // parts], w2_scales[:, :N // parts], grouped[:, H:H + N // parts])
+            hidden = turn.tile([P, C, TILES], BF16, name="hidden", align_bytes=64)
+            nc.vector.tensor_tensor(hidden[:], sil[:], accs[1][:].rearrange("p t c -> p c t"), MULT)
             if last:
-                vc = turn.tile([P, P], U32, name="v", bufs=2, align_bytes=64)
-                blocks[1] = vc[:]
-                quantise(vc[:], vs[:, P:], grp[:, H + P:])
-            hs = work.tile([P, C], U8, name="hs", align_bytes=64)
-            quantise(hc[:], hs[:], hb[:])
-            y = [psum.tile([P, NB // pieces, C], F32, name="y") for q in range(pieces)]
+                w2_blocks[1] = vector_ring([P, P], U32)[:]
+                quantise(w2_blocks[1], w2_scales[:, P:], grouped[:, H + P:])
+            h_scales = work.tile([P, C], U8, name="h_scales", align_bytes=64)
+            quantise(h_words[:], h_scales[:], hidden[:])
+            banks = [psum.tile([P, NB // parts, C], F32, name="y") for q in range(parts)]
             for b in range(NB):
                 nc.tensor.matmul_mx(
-                    out=y[b * pieces // NB][:, b % (NB // pieces), :],
-                    lhsT=blocks[b].bitcast(FP8X4),
-                    lhsT_scale=vs[:, P * b:P * b + P],
-                    rhs=hc[:].bitcast(FP8X4),
-                    rhs_scale=hs[:],
+                    out=banks[b * parts // NB][:, b % (NB // parts), :],
+                    lhsT=w2_blocks[b].bitcast(FP8X4),
+                    lhsT_scale=w2_scales[:, P * b:P * b + P],
+                    rhs=h_words[:].bitcast(FP8X4),
+                    rhs_scale=h_scales[:],
                     start=True,
                     stop=True,
                 )
-        way_back(E - 1, y, gates, NB)
+        way_back(E - 1, banks, gates)
         for b in range(NB):
             nc.sync.dma_start(out[P * b:P * b + P, :], wins[b][:])

@@ -96,8 +96,8 @@ def tile_routed_moe_kernel(tc, xT, w1, w3, w2, gate, offs, out):
                 )
 
         def interleave(grouped, raw, m):
-            src = raw.rearrange("p (j m t) -> p m j t", j=J, t=TILES)
-            dst = grouped.rearrange("p (t m) j -> p m j t", t=TILES)
+            src = raw.rearrange("p (u v m t) -> p m u t v", u=2, v=2, t=TILES)
+            dst = grouped.rearrange("p (t m) (u v) -> p m u t v", t=TILES, v=2)
             if m:
                 nc.vector.tensor_copy(dst[:, :m], src[:, :m])
             if m < P:

@@ -21,8 +21,8 @@ MULT = mybir.AluOpType.mult
 SILU = mybir.ActivationFunctionType.Silu
 
 WHOLE = 5
-V_SHARE = (0, 128, 0, 0, 64, 128)
-V_SHARE_LAST = (0, 0, 128, 64, 48, 64)
+V_SHARE = (0, 128, 0, 128, 0, 128)
+V_SHARE_LAST = (0, 0, 64, 64, 64, 64)
 
 FLOPS = 2 * S * (2 * K * H + H * N)
 
@@ -40,6 +40,7 @@ def tile_routed_moe_kernel(tc, xT, w1, w3, w2, gate, offs, out):
         turn = ctx.enter_context(tc.tile_pool(name="turn", bufs=1))
         wq = ctx.enter_context(tc.tile_pool(name="wq", bufs=2))
         work = ctx.enter_context(tc.tile_pool(name="work", bufs=2))
+        ends = ctx.enter_context(tc.tile_pool(name="ends", bufs=1))
         psum = ctx.enter_context(tc.psum_pool(name="psum", bufs=2))
 
         def quantise(words, scales, grouped):
@@ -83,16 +84,17 @@ def tile_routed_moe_kernel(tc, xT, w1, w3, w2, gate, offs, out):
         nc.vector.tensor_copy(slot_scales[:], token_scales[:].indirect(lst[:]))
         nc.sync.dma_start(gates_early[:], gate_rows[:, :, :S - C])
 
-        def first_layer(acc, words, scales, e, g, tiles):
+        def first_layer(accs, words, scales, e, g, tiles):
+            per_bank = TILES // len(accs)
             for t in tiles:
                 nc.tensor.matmul_mx(
-                    out=acc[:, t, :],
+                    out=accs[t // per_bank][:, t % per_bank, :],
                     lhsT=words[:, g, P * t:P * t + P].bitcast(FP8X4),
                     lhsT_scale=scales[:, g, P * t:P * t + P],
                     rhs=slot_words[:, g, C * e:C * e + C].bitcast(FP8X4),
                     rhs_scale=slot_scales[4 * g:, C * e:C * e + C],
-                    start=(g == 0 and t == 0),
-                    stop=(g == G - 1 and t == TILES - 1),
+                    start=(g == 0 and t % per_bank == 0),
+                    stop=(g == G - 1 and t % per_bank == per_bank - 1),
                 )
 
         def interleave(grouped, raw, m):
@@ -104,7 +106,7 @@ def tile_routed_moe_kernel(tc, xT, w1, w3, w2, gate, offs, out):
                 nc.scalar.copy(dst[:, m:], src[:, m:])
 
         def way_back(e, banks, gates):
-            gated = turn.tile([P, NB, C], F32, name="first" if 2 * (e + 1) >= WHOLE else "gated", align_bytes=64)
+            gated = turn.tile([P, NB, C], F32, name="gated", align_bytes=64)
             width = NB // len(banks)
             for q, bank in enumerate(banks):
                 blocks = slice(q * width, (q + 1) * width)
@@ -115,7 +117,9 @@ def tile_routed_moe_kernel(tc, xT, w1, w3, w2, gate, offs, out):
         for e in range(E):
             last = e == E - 1
             share = V_SHARE_LAST if last else V_SHARE
-            accs = [psum.tile([P, TILES, C], F32, name=f"acc{which}") for which in range(2)]
+            parts = 2 if last else 1
+            accs = [[psum.tile([P, TILES, C], F32, name="acc0")],
+                    [psum.tile([P, TILES // parts, C], F32, name=f"acc{1 + q}") for q in range(parts)]]
             words = [wq.tile([P, G, H], U32, name=f"words{which}", align_bytes=64) for which in range(2)]
             scales = [wq.tile([P, G, H], U8, name=f"scales{which}", align_bytes=64) for which in range(2)]
 
@@ -134,6 +138,8 @@ def tile_routed_moe_kernel(tc, xT, w1, w3, w2, gate, offs, out):
                     nc.sync.dma_start(raw[:], w_rows[which][e])
                 if i == 0:
                     grouped = turn.tile([P, H, J], BF16, name="first", align_bytes=64)
+                elif last and i == 2 * G - 2:
+                    grouped = ends.tile([P, H, J], BF16, name="fifth", offset=0, align_bytes=64)
                 elif share[i]:
                     grouped = vector_ring([P, H, J], BF16)
                 else:
@@ -146,7 +152,6 @@ def tile_routed_moe_kernel(tc, xT, w1, w3, w2, gate, offs, out):
                     way_back(e - 1, banks, gates)
 
             g = G - 1
-            parts = 2 if last else 1
             tail = rawp.tile([P, J * H + J * N + NB * C], F32, name="raw")
             if 2 * e + 1 >= WHOLE:
                 chunk = tail[:, :J * H]
@@ -172,34 +177,46 @@ def tile_routed_moe_kernel(tc, xT, w1, w3, w2, gate, offs, out):
                 finish(*pending)
                 for q in range(parts):
                     nc.vector.tensor_copy(dst[:, :, 2 * q:2 * q + 2, 2:], src[:, :, 2 * q:2 * q + 2, 2:])
-                sil = vector_ring([P, C, TILES], F32)
-                h_words = vector_ring([P, C], U32)
             else:
                 interleave(grouped[:, :H], chunk, share[-1])
                 finish(*pending)
-                sil = work.tile([P, C, TILES], F32, name="sil")
-                h_words = work.tile([P, C], U32, name="h_words", align_bytes=64)
-            nc.scalar.activation(sil[:], accs[0][:].rearrange("p t c -> p c t"), SILU)
+            pair = TILES // parts
+            if last:
+                sils = [ends.tile([P, C, pair], F32, name=f"sil{q}", offset=4 * C * pair * q, align_bytes=64) for q in range(parts)]
+            else:
+                sils = [work.tile([P, C, pair], F32, name="sil")]
+            for q in range(parts):
+                nc.scalar.activation(sils[q][:], accs[0][0][:, q * pair:(q + 1) * pair, :].rearrange("p t c -> p c t"), SILU)
             src, dst = by_lines(raw2, grouped[:, H:])
             width = N // LINE // parts
             for q in range(parts):
                 nc.scalar.copy(dst[:, q * width:(q + 1) * width], src[:, q * width:(q + 1) * width])
-            for q in range(parts):
-                cols = slice(q * H // parts, (q + 1) * H // parts)
+            steps = TILES if last else 1
+            for q in range(steps):
+                cols = slice(q * H // steps, (q + 1) * H // steps)
                 quantise(words[1][:, g, cols], scales[1][:, g, cols], grouped[:, cols, :])
-                first_layer(accs[1], words[1], scales[1], e, g, range(q * TILES // parts, (q + 1) * TILES // parts))
+                first_layer(accs[1], words[1], scales[1], e, g, range(q * TILES // steps, (q + 1) * TILES // steps))
 
             w2_scales = work.tile([P, N], U8, name="w2_scales", align_bytes=64)
-            w2_words = work.tile([P, N], U32, name="w2_words", align_bytes=64)
-            w2_blocks = [w2_words[:, P * b:P * b + P] for b in range(NB)]
-            quantise(w2_words[:, :N // parts], w2_scales[:, :N // parts], grouped[:, H:H + N // parts])
             hidden = turn.tile([P, C, TILES], BF16, name="hidden", align_bytes=64)
-            nc.vector.tensor_tensor(hidden[:], sil[:], accs[1][:].rearrange("p t c -> p c t"), MULT)
-            if last:
-                w2_blocks[1] = vector_ring([P, P], U32)[:]
-                quantise(w2_blocks[1], w2_scales[:, P:], grouped[:, H + P:])
+            h_words = work.tile([P, C], U32, name="h_words", align_bytes=64)
             h_scales = work.tile([P, C], U8, name="h_scales", align_bytes=64)
+            if not last:
+                w2_words = work.tile([P, N], U32, name="w2_words", align_bytes=64)
+                w2_blocks = [w2_words[:, P * b:P * b + P] for b in range(NB)]
+                quantise(w2_words[:], w2_scales[:], grouped[:, H:])
+            for q in range(parts):
+                nc.vector.tensor_tensor(
+                    hidden[:, :, q * pair:(q + 1) * pair], sils[q][:], accs[1][q][:].rearrange("p t c -> p c t"), MULT
+                )
+            if last:
+                block0 = ends.tile([P, P], U32, name="block0", offset=0, align_bytes=64)
+                quantise(block0[:], w2_scales[:, :P], grouped[:, H:H + P])
             quantise(h_words[:], h_scales[:], hidden[:])
+            if last:
+                block1 = turn.tile([P, P], U32, name="hidden", align_bytes=64)
+                quantise(block1[:], w2_scales[:, P:], grouped[:, H + P:])
+                w2_blocks = [block0[:], block1[:]]
             banks = [psum.tile([P, NB // parts, C], F32, name="y") for q in range(parts)]
             for b in range(NB):
                 nc.tensor.matmul_mx(

@@ -20,23 +20,27 @@ FP8X4 = mybir.dt.float8_e4m3fn_x4
 MULT = mybir.AluOpType.mult
 SILU = mybir.ActivationFunctionType.Silu
 
-WHOLE = 5
-V_SHARE = (0, 128, 0, 128, 0, 128)
-V_SHARE_LAST = (0, 0, 64, 64, 64, 64)
+LOADS = (((3,), (3,)), ((3,), (2, 1)), ((1, 1, 1), (1, 1, 1)), ((1, 1, 1), (1, 1, 1)))
+
+
+V_SHARE = ((0, 128, 0, 128, 0, 128), (0, 128, 0, 128, 0, 128), (0, 0, 64, 64, 64, 128), (0, 0, 64, 64, 64, 64))
+
+RING = 5
+SLOT_BYTES = 4 * G * J * H
 
 FLOPS = 2 * S * (2 * K * H + H * N)
 
 
 def tile_routed_moe_kernel(tc, xT, w1, w3, w2, gate, offs, out):
     nc = tc.nc
-    x_rows = xT.rearrange("(g p j) n -> g p (j n)", p=P, j=J)
+    x_rows = xT.rearrange("(g p j) n -> p g (j n)", p=P, j=J)
     w_rows = [w.rearrange("e (g p j) h -> e p g (j h)", p=P, j=J) for w in (w1, w3)]
     w2_rows = w2.rearrange("e (p j) n -> p e (j n)", j=J)
     gate_rows = gate.rearrange("(b p) s -> p b s", p=P)
 
     with ExitStack() as ctx:
         keep = ctx.enter_context(tc.tile_pool(name="keep", bufs=1))
-        rawp = ctx.enter_context(tc.tile_pool(name="rawp", bufs=5))
+        rawp = ctx.enter_context(tc.tile_pool(name="rawp", bufs=1))
         turn = ctx.enter_context(tc.tile_pool(name="turn", bufs=1))
         wq = ctx.enter_context(tc.tile_pool(name="wq", bufs=2))
         work = ctx.enter_context(tc.tile_pool(name="work", bufs=2))
@@ -45,6 +49,10 @@ def tile_routed_moe_kernel(tc, xT, w1, w3, w2, gate, offs, out):
 
         def quantise(words, scales, grouped):
             nc.vector.quantize_mx(out=words.bitcast(FP8X4), scales=scales, in_=grouped.rearrange("p c j -> p (c j)"))
+
+        def ring_tile(turn_number, shape):
+            slot = (2 + turn_number) % RING
+            return rawp.tile(shape, F32, name=f"raw{slot}", offset=slot * SLOT_BYTES, align_bytes=64)
 
         def vector_ring(shape, dtype):
             return turn.tile(shape, dtype, name="vector_ring", bufs=2, align_bytes=64)
@@ -67,15 +75,15 @@ def tile_routed_moe_kernel(tc, xT, w1, w3, w2, gate, offs, out):
         slot_scales = keep.tile([P, S], U8, name="slot_scales", align_bytes=64)
         token_scales = keep.tile([P, T], U8, name="token_scales", align_bytes=64)
         half = T // 2
+        xraw = rawp.tile([P, G, J * T], F32, name="xraw", offset=0, align_bytes=64)
         for g in range(G):
-            xraw = rawp.tile([P, J * T], F32, name="raw")
-            nc.sync.dma_start(xraw[:], x_rows[g])
+            nc.sync.dma_start(xraw[:, g], x_rows[:, g])
             if g == 0:
                 nc.sync.dma_start(lst[:], offs)
             token_words = turn.tile([P, T], U32, name=f"x{g + 1}", align_bytes=64)
             grouped = [turn.tile([P, half, J], BF16, name=f"x{g}", align_bytes=64), scalar_ring()]
             for u, copy in enumerate((nc.vector.tensor_copy, nc.scalar.copy)):
-                src = xraw[:].rearrange("p (j c i) -> p c j i", j=J, i=LINE)[:, u * half // LINE:(u + 1) * half // LINE]
+                src = xraw[:, g].rearrange("p (j c i) -> p c j i", j=J, i=LINE)[:, u * half // LINE:(u + 1) * half // LINE]
                 copy(grouped[u][:].rearrange("p (c i) j -> p c j i", i=LINE), src)
             for u in range(2):
                 tokens = slice(u * half, (u + 1) * half)
@@ -116,7 +124,7 @@ def tile_routed_moe_kernel(tc, xT, w1, w3, w2, gate, offs, out):
 
         for e in range(E):
             last = e == E - 1
-            share = V_SHARE_LAST if last else V_SHARE
+            share = V_SHARE[e]
             parts = 2 if last else 1
             accs = [[psum.tile([P, TILES, C], F32, name="acc0")],
                     [psum.tile([P, TILES // parts, C], F32, name=f"acc{1 + q}") for q in range(parts)]]
@@ -131,14 +139,15 @@ def tile_routed_moe_kernel(tc, xT, w1, w3, w2, gate, offs, out):
             for i in range(2 * G - 1):
                 which, g = divmod(i, G)
                 if g == 0:
-                    raw = rawp.tile([P, G, J * H], F32, name="raw")
-                if 2 * e + which >= WHOLE:
-                    nc.sync.dma_start(raw[:, g], w_rows[which][e, :, g])
-                elif g == 0:
-                    nc.sync.dma_start(raw[:], w_rows[which][e])
+                    raw = ring_tile(3 * e + which, [P, G, J * H])
+                    loaded = 0
+                    sizes = list(LOADS[e][which])
+                if g == loaded:
+                    loaded += sizes.pop(0)
+                    nc.sync.dma_start(raw[:, g:loaded], w_rows[which][e, :, g:loaded])
                 if i == 0:
                     grouped = turn.tile([P, H, J], BF16, name="first", align_bytes=64)
-                elif last and i == 2 * G - 2:
+                elif i == 2 * G - 2:
                     grouped = ends.tile([P, H, J], BF16, name="fifth", offset=0, align_bytes=64)
                 elif share[i]:
                     grouped = vector_ring([P, H, J], BF16)
@@ -152,8 +161,8 @@ def tile_routed_moe_kernel(tc, xT, w1, w3, w2, gate, offs, out):
                     way_back(e - 1, banks, gates)
 
             g = G - 1
-            tail = rawp.tile([P, J * H + J * N + NB * C], F32, name="raw")
-            if 2 * e + 1 >= WHOLE:
+            tail = ring_tile(3 * e + 2, [P, J * H + J * N + NB * C])
+            if loaded < G:
                 chunk = tail[:, :J * H]
                 width = J * H // parts
                 for q in range(parts):
@@ -181,10 +190,7 @@ def tile_routed_moe_kernel(tc, xT, w1, w3, w2, gate, offs, out):
                 interleave(grouped[:, :H], chunk, share[-1])
                 finish(*pending)
             pair = TILES // parts
-            if last:
-                sils = [ends.tile([P, C, pair], F32, name=f"sil{q}", offset=4 * C * pair * q, align_bytes=64) for q in range(parts)]
-            else:
-                sils = [work.tile([P, C, pair], F32, name="sil")]
+            sils = [ends.tile([P, C, pair], F32, name=f"sil{q}", offset=4 * C * pair * q, align_bytes=64) for q in range(parts)]
             for q in range(parts):
                 nc.scalar.activation(sils[q][:], accs[0][0][:, q * pair:(q + 1) * pair, :].rearrange("p t c -> p c t"), SILU)
             src, dst = by_lines(raw2, grouped[:, H:])

@@ -50,9 +50,9 @@ def tile_routed_moe_kernel(tc, xT, w1, w3, w2, gate, offs, out):
         def quantise(words, scales, grouped):
             nc.vector.quantize_mx(out=words.bitcast(FP8X4), scales=scales, in_=grouped.rearrange("p c j -> p (c j)"))
 
-        def ring_tile(turn_number, shape):
+        def ring_tile(turn_number, shape, dtype=F32, name="raw", start=0):
             slot = (2 + turn_number) % RING
-            return rawp.tile(shape, F32, name=f"raw{slot}", offset=slot * SLOT_BYTES, align_bytes=64)
+            return rawp.tile(shape, dtype, name=f"{name}{slot}", offset=slot * SLOT_BYTES + start, align_bytes=64)
 
         def vector_ring(shape, dtype):
             return turn.tile(shape, dtype, name="vector_ring", bufs=2, align_bytes=64)
@@ -113,8 +113,7 @@ def tile_routed_moe_kernel(tc, xT, w1, w3, w2, gate, offs, out):
             if m < P:
                 nc.scalar.copy(dst[:, m:], src[:, m:])
 
-        def way_back(e, banks, gates):
-            gated = turn.tile([P, NB, C], F32, name="gated", align_bytes=64)
+        def way_back(e, banks, gates, gated):
             width = NB // len(banks)
             for q, bank in enumerate(banks):
                 blocks = slice(q * width, (q + 1) * width)
@@ -139,12 +138,19 @@ def tile_routed_moe_kernel(tc, xT, w1, w3, w2, gate, offs, out):
             for i in range(2 * G - 1):
                 which, g = divmod(i, G)
                 if g == 0:
-                    raw = ring_tile(3 * e + which, [P, G, J * H])
+                    if not (last and which == 1):
+                        raw = ring_tile(3 * e + which, [P, G, J * H])
                     loaded = 0
                     sizes = list(LOADS[e][which])
-                if g == loaded:
-                    loaded += sizes.pop(0)
-                    nc.sync.dma_start(raw[:, g:loaded], w_rows[which][e, :, g:loaded])
+                if last and which == 1:
+                    loaded += 1
+                    rows = ring_tile(3 * e + which, [P, J * H], name=f"own{g}_", start=4 * J * H * g)[:]
+                    nc.sync.dma_start(rows, w_rows[which][e, :, g])
+                else:
+                    rows = raw[:, g]
+                    if g == loaded:
+                        loaded += sizes.pop(0)
+                        nc.sync.dma_start(raw[:, g:loaded], w_rows[which][e, :, g:loaded])
                 if i == 0:
                     grouped = turn.tile([P, H, J], BF16, name="first", align_bytes=64)
                 elif i == 2 * G - 2:
@@ -153,26 +159,26 @@ def tile_routed_moe_kernel(tc, xT, w1, w3, w2, gate, offs, out):
                     grouped = vector_ring([P, H, J], BF16)
                 else:
                     grouped = scalar_ring()
-                interleave(grouped[:], raw[:, g], share[i])
+                interleave(grouped[:], rows, share[i])
                 if pending:
                     finish(*pending)
                 pending = (which, g, grouped[:])
                 if i == 1 and e > 0:
-                    way_back(e - 1, banks, gates)
+                    way_back(e - 1, banks, gates, turn.tile([P, NB, C], F32, name="gated", align_bytes=64))
 
             g = G - 1
-            tail = ring_tile(3 * e + 2, [P, J * H + J * N + NB * C])
+            tail = ring_tile(3 * e + 2, [P, J * N + NB * C], name="tail", start=4 * J * H)
             if loaded < G:
-                chunk = tail[:, :J * H]
+                chunk = ring_tile(3 * e + 2, [P, J * H])[:]
                 width = J * H // parts
                 for q in range(parts):
                     nc.sync.dma_start(chunk[:, q * width:(q + 1) * width], w_rows[1][e, :, g, q * width:(q + 1) * width])
             else:
                 chunk = raw[:, g]
-            raw2 = tail[:, J * H:J * H + J * N]
+            raw2 = tail[:, :J * N]
             nc.sync.dma_start(raw2, w2_rows[:, e])
             if last:
-                gates = tail[:, J * H + J * N:].rearrange("p (b s) -> p b s", b=NB)
+                gates = tail[:, J * N:].rearrange("p (b s) -> p b s", b=NB)
                 nc.sync.dma_start(gates, gate_rows[:, :, S - C:])
             else:
                 gates = gates_early[:, :, C * e:C * e + C]
@@ -184,19 +190,27 @@ def tile_routed_moe_kernel(tc, xT, w1, w3, w2, gate, offs, out):
                 nc.vector.tensor_copy(dst[:, :m, :, :2], src[:, :m, :, :2])
                 nc.scalar.copy(dst[:, m:, :, :2], src[:, m:, :, :2])
                 finish(*pending)
-                for q in range(parts):
-                    nc.vector.tensor_copy(dst[:, :, 2 * q:2 * q + 2, 2:], src[:, :, 2 * q:2 * q + 2, 2:])
+                for t in range(2):
+                    nc.vector.tensor_copy(dst[:, :, t, 2:], src[:, :, t, 2:])
+                nc.scalar.copy(dst[:, :, 2:, 2:], src[:, :, 2:, 2:])
             else:
                 interleave(grouped[:, :H], chunk, share[-1])
                 finish(*pending)
             pair = TILES // parts
-            sils = [ends.tile([P, C, pair], F32, name=f"sil{q}", offset=4 * C * pair * q, align_bytes=64) for q in range(parts)]
+            if last:
+                sils = [ring_tile(3 * e + 1, [P, C, pair], name=f"sil{q}_", start=4 * C * pair * q) for q in range(parts)]
+            else:
+                sils = [ends.tile([P, C, pair], F32, name="sil", offset=0, align_bytes=64)]
             for q in range(parts):
                 nc.scalar.activation(sils[q][:], accs[0][0][:, q * pair:(q + 1) * pair, :].rearrange("p t c -> p c t"), SILU)
-            src, dst = by_lines(raw2, grouped[:, H:])
+            if last:
+                w2_grouped = [ends.tile([P, P, J], BF16, name=f"w2_grouped{b}", offset=2 * J * (H + P * b), align_bytes=64)[:] for b in range(NB)]
+            else:
+                w2_grouped = [grouped[:, H:]]
+            src = raw2.rearrange("p (j c i) -> p c j i", j=J, i=LINE)
             width = N // LINE // parts
             for q in range(parts):
-                nc.scalar.copy(dst[:, q * width:(q + 1) * width], src[:, q * width:(q + 1) * width])
+                nc.scalar.copy(w2_grouped[q].rearrange("p (c i) j -> p c j i", i=LINE), src[:, q * width:(q + 1) * width])
             steps = TILES if last else 1
             for q in range(steps):
                 cols = slice(q * H // steps, (q + 1) * H // steps)
@@ -205,7 +219,10 @@ def tile_routed_moe_kernel(tc, xT, w1, w3, w2, gate, offs, out):
 
             w2_scales = work.tile([P, N], U8, name="w2_scales", align_bytes=64)
             hidden = turn.tile([P, C, TILES], BF16, name="hidden", align_bytes=64)
-            h_words = work.tile([P, C], U32, name="h_words", align_bytes=64)
+            if last:
+                h_words = ends.tile([P, C], U32, name="h_words_last", offset=2 * J * H, align_bytes=64)
+            else:
+                h_words = work.tile([P, C], U32, name="h_words", align_bytes=64)
             h_scales = work.tile([P, C], U8, name="h_scales", align_bytes=64)
             if not last:
                 w2_words = work.tile([P, N], U32, name="w2_words", align_bytes=64)
@@ -216,12 +233,12 @@ def tile_routed_moe_kernel(tc, xT, w1, w3, w2, gate, offs, out):
                     hidden[:, :, q * pair:(q + 1) * pair], sils[q][:], accs[1][q][:].rearrange("p t c -> p c t"), MULT
                 )
             if last:
-                block0 = ends.tile([P, P], U32, name="block0", offset=0, align_bytes=64)
-                quantise(block0[:], w2_scales[:, :P], grouped[:, H:H + P])
+                block0 = ring_tile(3 * e + 1, [P, P], U32, name="block0_")
+                quantise(block0[:], w2_scales[:, :P], w2_grouped[0])
             quantise(h_words[:], h_scales[:], hidden[:])
             if last:
                 block1 = turn.tile([P, P], U32, name="hidden", align_bytes=64)
-                quantise(block1[:], w2_scales[:, P:], grouped[:, H + P:])
+                quantise(block1[:], w2_scales[:, P:], w2_grouped[1])
                 w2_blocks = [block0[:], block1[:]]
             banks = [psum.tile([P, NB // parts, C], F32, name="y") for q in range(parts)]
             for b in range(NB):
@@ -234,6 +251,6 @@ def tile_routed_moe_kernel(tc, xT, w1, w3, w2, gate, offs, out):
                     start=True,
                     stop=True,
                 )
-        way_back(E - 1, banks, gates)
+        way_back(E - 1, banks, gates, ends.tile([P, NB, C], F32, name="gated_last", offset=2 * J * (H + P), align_bytes=64))
         for b in range(NB):
             nc.sync.dma_start(out[P * b:P * b + P, :], wins[b][:])

@@ -25,6 +25,7 @@ LOADS = (((3,), (3,)), ((3,), (2, 1)), ((1, 1, 1), (1, 1, 1)), ((1, 1, 1), (1, 1
 
 V_SHARE = ((0, 128, 0, 128, 0, 128), (0, 128, 0, 128, 0, 128), (0, 0, 64, 64, 64, 128), (0, 0, 64, 64, 64, 64))
 
+BURST = 256
 RING = 5
 SLOT_BYTES = 4 * G * J * H
 
@@ -52,7 +53,7 @@ def tile_routed_moe_kernel(tc, xT, w1, w3, w2, gate, offs, out):
 
         def ring_tile(turn_number, shape, dtype=F32, name="raw", start=0):
             slot = (2 + turn_number) % RING
-            return rawp.tile(shape, dtype, name=f"{name}{slot}", offset=slot * SLOT_BYTES + start, align_bytes=64)
+            return rawp.tile(shape, dtype, name=f"{name}{slot}", offset=slot * SLOT_BYTES + start, align_bytes=BURST)
 
         def vector_ring(shape, dtype):
             return turn.tile(shape, dtype, name="vector_ring", bufs=2, align_bytes=64)
@@ -64,10 +65,10 @@ def tile_routed_moe_kernel(tc, xT, w1, w3, w2, gate, offs, out):
             return raw.rearrange("p (j c i) -> p c j i", j=J, i=LINE), grouped.rearrange("p (c i) j -> p c j i", i=LINE)
 
         lst = keep.tile([P, S // 16], U16, name="lst")
-        gates_early = keep.tile([P, NB, S - C], F32, name="gates_early")
+        gates_early = keep.tile([P, NB, S - C], F32, name="gates_early", align_bytes=BURST)
         wins = []
         for b in range(NB):
-            win = keep.tile([P, T], F32, name=f"win{b}")
+            win = keep.tile([P, T], F32, name=f"win{b}", align_bytes=BURST)
             nc.vector.memset(win[:], 0.0)
             wins.append(win)
 
@@ -75,7 +76,7 @@ def tile_routed_moe_kernel(tc, xT, w1, w3, w2, gate, offs, out):
         slot_scales = keep.tile([P, S], U8, name="slot_scales", align_bytes=64)
         token_scales = keep.tile([P, T], U8, name="token_scales", align_bytes=64)
         half = T // 2
-        xraw = rawp.tile([P, G, J * T], F32, name="xraw", offset=0, align_bytes=64)
+        xraw = rawp.tile([P, G, J * T], F32, name="xraw", offset=0, align_bytes=BURST)
         for g in range(G):
             nc.sync.dma_start(xraw[:, g], x_rows[:, g])
             if g == 0:

@@ -25,7 +25,7 @@ LOADS = (((3,), (3,)), ((3,), (2, 1)), ((1, 1, 1), (1, 1, 1)), ((1, 1, 1), (1, 1
 
 V_SHARE = ((0, 128, 0, 128, 0, 128), (0, 128, 0, 128, 0, 128), (0, 0, 64, 64, 64, 128), (0, 0, 64, 64, 64, 64))
 
-BURST = 256
+BURST = 4096
 RING = 5
 SLOT_BYTES = 4 * G * J * H
 
@@ -51,9 +51,9 @@ def tile_routed_moe_kernel(tc, xT, w1, w3, w2, gate, offs, out):
         def quantise(words, scales, grouped):
             nc.vector.quantize_mx(out=words.bitcast(FP8X4), scales=scales, in_=grouped.rearrange("p c j -> p (c j)"))
 
-        def ring_tile(turn_number, shape, dtype=F32, name="raw", start=0):
+        def ring_tile(turn_number, shape, dtype=F32, name="raw", start=0, align=BURST):
             slot = (2 + turn_number) % RING
-            return rawp.tile(shape, dtype, name=f"{name}{slot}", offset=slot * SLOT_BYTES + start, align_bytes=BURST)
+            return rawp.tile(shape, dtype, name=f"{name}{slot}", offset=slot * SLOT_BYTES + start, align_bytes=align)
 
         def vector_ring(shape, dtype):
             return turn.tile(shape, dtype, name="vector_ring", bufs=2, align_bytes=64)
@@ -64,13 +64,13 @@ def tile_routed_moe_kernel(tc, xT, w1, w3, w2, gate, offs, out):
         def by_lines(raw, grouped):
             return raw.rearrange("p (j c i) -> p c j i", j=J, i=LINE), grouped.rearrange("p (c i) j -> p c j i", i=LINE)
 
-        lst = keep.tile([P, S // 16], U16, name="lst")
-        gates_early = keep.tile([P, NB, S - C], F32, name="gates_early", align_bytes=BURST)
         wins = []
         for b in range(NB):
             win = keep.tile([P, T], F32, name=f"win{b}", align_bytes=BURST)
             nc.vector.memset(win[:], 0.0)
             wins.append(win)
+        gates_early = keep.tile([P, NB, S - C], F32, name="gates_early", align_bytes=256)
+        lst = keep.tile([P, S // 16], U16, name="lst")
 
         slot_words = keep.tile([P, G, S], U32, name="slot_words", align_bytes=64)
         slot_scales = keep.tile([P, S], U8, name="slot_scales", align_bytes=64)
@@ -199,7 +199,7 @@ def tile_routed_moe_kernel(tc, xT, w1, w3, w2, gate, offs, out):
                 finish(*pending)
             pair = TILES // parts
             if last:
-                sils = [ring_tile(3 * e + 1, [P, C, pair], name=f"sil{q}_", start=4 * C * pair * q) for q in range(parts)]
+                sils = [ring_tile(3 * e + 1, [P, C, pair], name=f"sil{q}_", start=4 * C * pair * q, align=64) for q in range(parts)]
             else:
                 sils = [ends.tile([P, C, pair], F32, name="sil", offset=0, align_bytes=64)]
             for q in range(parts):

@@ -20,7 +20,7 @@ FP8X4 = mybir.dt.float8_e4m3fn_x4
 MULT = mybir.AluOpType.mult
 SILU = mybir.ActivationFunctionType.Silu
 
-LOADS = (((3,), (3,)), ((3,), (2, 1)), ((1, 1, 1), (1, 1, 1)), ((1, 1, 1), (1, 1, 1)))
+LOADS = (((1, 1, 1), (1, 1, 1)), ((1, 1, 1), (1, 1, 1)), ((1, 1, 1), (1, 1, 1)), ((1, 1, 1), (1, 1, 1)))
 
 
 V_SHARE = ((0, 128, 0, 128, 0, 128), (0, 128, 0, 128, 0, 128), (0, 0, 64, 64, 64, 128), (0, 0, 64, 64, 64, 64))
@@ -91,7 +91,6 @@ def tile_routed_moe_kernel(tc, xT, w1, w3, w2, gate, offs, out):
                 quantise(token_words[:, tokens], token_scales[4 * g:, tokens], grouped[u][:])
             nc.vector.tensor_copy(slot_words[:, g, :], token_words[:].indirect(lst[:]))
         nc.vector.tensor_copy(slot_scales[:], token_scales[:].indirect(lst[:]))
-        nc.sync.dma_start(gates_early[:], gate_rows[:, :, :S - C])
 
         def first_layer(accs, words, scales, e, g, tiles):
             per_bank = TILES // len(accs)
@@ -178,6 +177,8 @@ def tile_routed_moe_kernel(tc, xT, w1, w3, w2, gate, offs, out):
                 chunk = raw[:, g]
             raw2 = tail[:, :J * N]
             nc.sync.dma_start(raw2, w2_rows[:, e])
+            if e == 0:
+                nc.sync.dma_start(gates_early[:], gate_rows[:, :, :S - C])
             if last:
                 gates = tail[:, J * N:].rearrange("p (b s) -> p b s", b=NB)
                 nc.sync.dma_start(gates, gate_rows[:, :, S - C:])

@@ -20,10 +20,10 @@ FP8X4 = mybir.dt.float8_e4m3fn_x4
 MULT = mybir.AluOpType.mult
 SILU = mybir.ActivationFunctionType.Silu
 
-LOADS = (((1, 1, 1), (1, 1, 1)), ((1, 1, 1), (1, 1, 1)), ((1, 1, 1), (1, 1, 1)), ((1, 1, 1), (1, 1, 1)))
+LOADS = (((3,), (2, 1)), ((2, 1), (2, 1)), ((1, 1, 1), (1, 1, 1)), ((1, 1, 1), (1, 1, 1)))
 
 
-V_SHARE = ((0, 128, 0, 128, 0, 128), (0, 128, 0, 128, 0, 128), (0, 0, 64, 64, 64, 128), (0, 0, 64, 64, 64, 64))
+V_SHARE = ((128, 0, 64, 128, 0, 128), (0, 128, 0, 128, 0, 128), (0, 0, 64, 64, 64, 128), (0, 0, 32, 64, 80, 64))
 
 BURST = 4096
 RING = 5
@@ -151,6 +151,15 @@ def tile_routed_moe_kernel(tc, xT, w1, w3, w2, gate, offs, out):
                     if g == loaded:
                         loaded += sizes.pop(0)
                         nc.sync.dma_start(raw[:, g:loaded], w_rows[which][e, :, g:loaded])
+                if last and i == 0:
+                    src = rows.rearrange("p (u v m t) -> p m u t v", u=2, v=2, t=TILES)
+                    for q, (name, copy) in enumerate((("first", nc.scalar.copy), ("hidden", nc.vector.tensor_copy))):
+                        grouped = turn.tile([P, H // 2, J], BF16, name=name, align_bytes=64)
+                        copy(grouped[:].rearrange("p (t m) (u v) -> p m u t v", t=2, v=2), src[:, :, :, 2 * q:2 * q + 2])
+                        cols = slice(q * H // 2, (q + 1) * H // 2)
+                        quantise(words[0][:, 0, cols], scales[0][:, 0, cols], grouped[:])
+                        first_layer(accs[0], words[0], scales[0], e, 0, range(2 * q, 2 * q + 2))
+                    continue
                 if i == 0:
                     grouped = turn.tile([P, H, J], BF16, name="first", align_bytes=64)
                 elif i == 2 * G - 2:

@@ -98,7 +98,7 @@ def tile_routed_moe_kernel(tc, xT, w1, w3, w2, gate, offs, out):
                 nc.tensor.matmul_mx(
                     out=accs[t // per_bank][:, t % per_bank, :],
                     lhsT=words[:, g, P * t:P * t + P].bitcast(FP8X4),
-                    lhsT_scale=scales[:, g, P * t:P * t + P],
+                    lhsT_scale=scales(g, slice(P * t, P * t + P)),
                     rhs=slot_words[:, g, C * e:C * e + C].bitcast(FP8X4),
                     rhs_scale=slot_scales[4 * g:, C * e:C * e + C],
                     start=(g == 0 and t % per_bank == 0),
@@ -128,11 +128,18 @@ def tile_routed_moe_kernel(tc, xT, w1, w3, w2, gate, offs, out):
             accs = [[psum.tile([P, TILES, C], F32, name="acc0")],
                     [psum.tile([P, TILES // parts, C], F32, name=f"acc{1 + q}") for q in range(parts)]]
             words = [wq.tile([P, G, H], U32, name=f"words{which}", align_bytes=64) for which in range(2)]
-            scales = [wq.tile([P, G, H], U8, name=f"scales{which}", align_bytes=64) for which in range(2)]
+            planes = [wq.tile([P, G, H], U8, name=f"scales{which}", align_bytes=64) for which in range(2)]
+            scales = [lambda g, cols: planes[0][:, g, cols], lambda g, cols: planes[1][:, g, cols]]
+            if last:
+                scales[1] = lambda g, cols: planes[1][4 * (g % 2):, g // 2, cols]
 
             def finish(which, g, grouped):
-                quantise(words[which][:, g], scales[which][:, g], grouped)
-                first_layer(accs[which], words[which], scales[which], e, g, range(TILES))
+                quantise(words[which][:, g], scales[which](g, slice(0, H)), grouped)
+                if last and which == 1:
+                    for back in range(2 * g):
+                        first_layer(accs[which], words[which], scales[which], e, back, range(TILES))
+                else:
+                    first_layer(accs[which], words[which], scales[which], e, g, range(TILES))
 
             pending = None
             for i in range(2 * G - 1):
@@ -157,7 +164,7 @@ def tile_routed_moe_kernel(tc, xT, w1, w3, w2, gate, offs, out):
                         grouped = turn.tile([P, H // 2, J], BF16, name=name, align_bytes=64)
                         copy(grouped[:].rearrange("p (t m) (u v) -> p m u t v", t=2, v=2), src[:, :, :, 2 * q:2 * q + 2])
                         cols = slice(q * H // 2, (q + 1) * H // 2)
-                        quantise(words[0][:, 0, cols], scales[0][:, 0, cols], grouped[:])
+                        quantise(words[0][:, 0, cols], scales[0](0, cols), grouped[:])
                         first_layer(accs[0], words[0], scales[0], e, 0, range(2 * q, 2 * q + 2))
                     continue
                 if i == 0:
@@ -225,7 +232,7 @@ def tile_routed_moe_kernel(tc, xT, w1, w3, w2, gate, offs, out):
             steps = TILES if last else 1
             for q in range(steps):
                 cols = slice(q * H // steps, (q + 1) * H // steps)
-                quantise(words[1][:, g, cols], scales[1][:, g, cols], grouped[:, cols, :])
+                quantise(words[1][:, g, cols], scales[1](g, cols), grouped[:, cols, :])
                 first_layer(accs[1], words[1], scales[1], e, g, range(q * TILES // steps, (q + 1) * TILES // steps))
 
             w2_scales = work.tile([P, N], U8, name="w2_scales", align_bytes=64)

@@ -19,15 +19,13 @@ U8 = mybir.dt.uint8
 FP8X4 = mybir.dt.float8_e4m3fn_x4
 MULT = mybir.AluOpType.mult
 SILU = mybir.ActivationFunctionType.Silu
+COPY = mybir.ActivationFunctionType.Copy
 
-LOADS = (((3,), (2, 1)), ((2, 1), (2, 1)), ((1, 1, 1), (1, 1, 1)), ((1, 1, 1), (1, 1, 1)))
-
-
-V_SHARE = ((128, 0, 64, 128, 0, 128), (0, 128, 0, 128, 0, 128), (0, 0, 64, 64, 64, 128), (0, 0, 32, 64, 80, 64))
-
+LATE = 2
 BURST = 4096
-RING = 5
-SLOT_BYTES = 4 * G * J * H
+RING_BYTES = 16 * BURST
+SHARE = 48
+EVEN_SHARE = 80
 
 FLOPS = 2 * S * (2 * K * H + H * N)
 
@@ -41,56 +39,53 @@ def tile_routed_moe_kernel(tc, xT, w1, w3, w2, gate, offs, out):
 
     with ExitStack() as ctx:
         keep = ctx.enter_context(tc.tile_pool(name="keep", bufs=1))
-        rawp = ctx.enter_context(tc.tile_pool(name="rawp", bufs=1))
-        turn = ctx.enter_context(tc.tile_pool(name="turn", bufs=1))
-        wq = ctx.enter_context(tc.tile_pool(name="wq", bufs=2))
+        ring = ctx.enter_context(tc.tile_pool(name="ring", bufs=1))
         work = ctx.enter_context(tc.tile_pool(name="work", bufs=2))
-        ends = ctx.enter_context(tc.tile_pool(name="ends", bufs=1))
         psum = ctx.enter_context(tc.psum_pool(name="psum", bufs=2))
+
+        ends = [0]
+
+        def load(source, shape):
+            size = -(-4 * shape[1] * (shape[2] if len(shape) > 2 else 1) // BURST) * BURST
+            start = ends[-1] if ends[-1] + size <= RING_BYTES else 0
+            ends.append(start + size)
+            raw = ring.tile(shape, F32, name=f"raw{len(ends)}", offset=start, align_bytes=BURST)
+            nc.sync.dma_start(raw[:], source)
+            return raw
 
         def quantise(words, scales, grouped):
             nc.vector.quantize_mx(out=words.bitcast(FP8X4), scales=scales, in_=grouped.rearrange("p c j -> p (c j)"))
 
-        def ring_tile(turn_number, shape, dtype=F32, name="raw", start=0, align=BURST):
-            slot = (2 + turn_number) % RING
-            return rawp.tile(shape, dtype, name=f"{name}{slot}", offset=slot * SLOT_BYTES + start, align_bytes=align)
-
-        def vector_ring(shape, dtype):
-            return turn.tile(shape, dtype, name="vector_ring", bufs=2, align_bytes=64)
-
-        def scalar_ring():
-            return turn.tile([P, H, J], BF16, name="scalar_ring", bufs=3, align_bytes=64)
-
-        def by_lines(raw, grouped):
-            return raw.rearrange("p (j c i) -> p c j i", j=J, i=LINE), grouped.rearrange("p (c i) j -> p c j i", i=LINE)
+        def staging():
+            return work.tile([P, H, J], BF16, name="staging", bufs=6, align_bytes=64)
 
         wins = []
         for b in range(NB):
             win = keep.tile([P, T], F32, name=f"win{b}", align_bytes=BURST)
             nc.vector.memset(win[:], 0.0)
             wins.append(win)
-        gates_early = keep.tile([P, NB, S - C], F32, name="gates_early", align_bytes=256)
         lst = keep.tile([P, S // 16], U16, name="lst")
 
         slot_words = keep.tile([P, G, S], U32, name="slot_words", align_bytes=64)
         slot_scales = keep.tile([P, S], U8, name="slot_scales", align_bytes=64)
         token_scales = keep.tile([P, T], U8, name="token_scales", align_bytes=64)
         half = T // 2
-        xraw = rawp.tile([P, G, J * T], F32, name="xraw", offset=0, align_bytes=BURST)
         for g in range(G):
-            nc.sync.dma_start(xraw[:, g], x_rows[:, g])
+            xraw = load(x_rows[:, g], [P, J * T])
             if g == 0:
                 nc.sync.dma_start(lst[:], offs)
-            token_words = turn.tile([P, T], U32, name=f"x{g + 1}", align_bytes=64)
-            grouped = [turn.tile([P, half, J], BF16, name=f"x{g}", align_bytes=64), scalar_ring()]
+            token_words = work.tile([P, T], U32, name="token_words", align_bytes=64)
+            src = xraw[:].rearrange("p (j c i) -> p c j i", j=J, i=LINE)
             for u, copy in enumerate((nc.vector.tensor_copy, nc.scalar.copy)):
-                src = xraw[:, g].rearrange("p (j c i) -> p c j i", j=J, i=LINE)[:, u * half // LINE:(u + 1) * half // LINE]
-                copy(grouped[u][:].rearrange("p (c i) j -> p c j i", i=LINE), src)
-            for u in range(2):
+                grouped = staging()
+                copy(grouped[:].rearrange("p (c i) j -> p c j i", i=LINE), src[:, u * half // LINE:(u + 1) * half // LINE])
                 tokens = slice(u * half, (u + 1) * half)
-                quantise(token_words[:, tokens], token_scales[4 * g:, tokens], grouped[u][:])
+                quantise(token_words[:, tokens], token_scales[4 * g:, tokens], grouped[:])
             nc.vector.tensor_copy(slot_words[:, g, :], token_words[:].indirect(lst[:]))
         nc.vector.tensor_copy(slot_scales[:], token_scales[:].indirect(lst[:]))
+
+        early = (E - LATE) * C
+        gates_early = keep.tile([P, NB, early], F32, name="gates_early", align_bytes=256)
 
         def first_layer(accs, words, scales, e, g, tiles):
             per_bank = TILES // len(accs)
@@ -113,162 +108,145 @@ def tile_routed_moe_kernel(tc, xT, w1, w3, w2, gate, offs, out):
             if m < P:
                 nc.scalar.copy(dst[:, m:], src[:, m:])
 
-        def way_back(e, banks, gates, gated):
-            width = NB // len(banks)
-            for q, bank in enumerate(banks):
-                blocks = slice(q * width, (q + 1) * width)
-                nc.vector.tensor_tensor(gated[:, blocks, :], bank[:], gates[:, blocks, :], MULT)
-            for b in range(NB):
-                nc.vector.tensor_copy(wins[b][:].indirect(lst[:, e * C // 16:(e + 1) * C // 16]), gated[:, b, :])
+        def w2_interleave(raw, blocks, state, copy=nc.scalar.copy):
+            cols = slice(P * blocks[0], P * blocks[-1] + P)
+            src = raw[:].rearrange("p (j c i) -> p c j i", j=J, i=LINE)
+            copy(state[0][:, cols].rearrange("p (c i) j -> p c j i", i=LINE), src[:, cols.start // LINE:cols.stop // LINE])
 
+        def w2_quantise(blocks, state):
+            grouped, words, scales = state
+            cols = slice(P * blocks[0], P * blocks[-1] + P)
+            quantise(words[:, cols], scales[:, cols], grouped[:, cols])
+
+        def w2_tiles():
+            return (work.tile([P, N, J], BF16, name="w2_grouped", align_bytes=64),
+                    work.tile([P, N], U32, name="w2_words", align_bytes=64),
+                    work.tile([P, N], U8, name="w2_scales", align_bytes=64))
+
+        def second_layer(state, hq, blocks):
+            bank = psum.tile([P, len(blocks), C], F32, name="y", bufs=4)
+            for q, b in enumerate(blocks):
+                nc.tensor.matmul_mx(
+                    out=bank[:, q, :],
+                    lhsT=state[1][:, P * b:P * b + P].bitcast(FP8X4),
+                    lhsT_scale=state[2][:, P * b:P * b + P],
+                    rhs=hq[0][:].bitcast(FP8X4),
+                    rhs_scale=hq[1][:],
+                    start=True,
+                    stop=True,
+                )
+            return bank
+
+        def gated_sums(bank, gates, blocks):
+            gated = work.tile([P, len(blocks), C], F32, name="gated", bufs=4, align_bytes=64)
+            nc.vector.tensor_tensor(gated[:], bank[:], gates[:, blocks[0]:blocks[-1] + 1, :], MULT)
+            return gated
+
+        def scatter(e, b, values, on_scalar=False):
+            window = wins[b][:].indirect(lst[:, e * C // 16:(e + 1) * C // 16])
+            if on_scalar:
+                nc.scalar.activation(window, values, COPY)
+            else:
+                nc.vector.tensor_copy(window, values)
+
+        hidden_codes = []
+        both = range(NB)
         for e in range(E):
             last = e == E - 1
-            share = V_SHARE[e]
-            parts = 2 if last else 1
-            accs = [[psum.tile([P, TILES, C], F32, name="acc0")],
-                    [psum.tile([P, TILES // parts, C], F32, name=f"acc{1 + q}") for q in range(parts)]]
-            words = [wq.tile([P, G, H], U32, name=f"words{which}", align_bytes=64) for which in range(2)]
-            planes = [wq.tile([P, G, H], U8, name=f"scales{which}", align_bytes=64) for which in range(2)]
+            parts = 1
+            pair = TILES // parts
+            accs = [[psum.tile([P, TILES, C], F32, name="acc0", bufs=1)],
+                    [psum.tile([P, pair, C], F32, name=f"acc{1 + q}", bufs=2 - q) for q in range(parts)]]
+            words = [work.tile([P, G, H], U32, name=f"words{which}", align_bytes=64) for which in range(2)]
+            planes = [work.tile([P, G, H], U8, name=f"scales{which}", align_bytes=64) for which in range(2)]
             scales = [lambda g, cols: planes[0][:, g, cols], lambda g, cols: planes[1][:, g, cols]]
             if last:
                 scales[1] = lambda g, cols: planes[1][4 * (g % 2):, g // 2, cols]
-
-            def finish(which, g, grouped):
-                quantise(words[which][:, g], scales[which](g, slice(0, H)), grouped)
+            sils = []
+            for i in range(2 * G - (1 if last else 0)):
+                which, g = divmod(i, G)
+                raw = load(w_rows[which][e, :, g], [P, J * H])
+                grouped = staging()
+                share = 0 if (e == 0 and i < 2) else EVEN_SHARE if (last and i == 2 * G - 2) else SHARE
+                interleave(grouped[:], raw[:], share)
+                quantise(words[which][:, g], scales[which](g, slice(0, H)), grouped[:])
                 if last and which == 1:
                     for back in range(2 * g):
                         first_layer(accs[which], words[which], scales[which], e, back, range(TILES))
                 else:
                     first_layer(accs[which], words[which], scales[which], e, g, range(TILES))
-
-            pending = None
-            for i in range(2 * G - 1):
-                which, g = divmod(i, G)
-                if g == 0:
-                    if not (last and which == 1):
-                        raw = ring_tile(3 * e + which, [P, G, J * H])
-                    loaded = 0
-                    sizes = list(LOADS[e][which])
-                if last and which == 1:
-                    loaded += 1
-                    rows = ring_tile(3 * e + which, [P, J * H], name=f"own{g}_", start=4 * J * H * g)[:]
-                    nc.sync.dma_start(rows, w_rows[which][e, :, g])
-                else:
-                    rows = raw[:, g]
-                    if g == loaded:
-                        loaded += sizes.pop(0)
-                        nc.sync.dma_start(raw[:, g:loaded], w_rows[which][e, :, g:loaded])
-                if last and i == 0:
-                    src = rows.rearrange("p (u v m t) -> p m u t v", u=2, v=2, t=TILES)
-                    for q, (name, copy) in enumerate((("first", nc.scalar.copy), ("hidden", nc.vector.tensor_copy))):
-                        grouped = turn.tile([P, H // 2, J], BF16, name=name, align_bytes=64)
-                        copy(grouped[:].rearrange("p (t m) (u v) -> p m u t v", t=2, v=2), src[:, :, :, 2 * q:2 * q + 2])
-                        cols = slice(q * H // 2, (q + 1) * H // 2)
-                        quantise(words[0][:, 0, cols], scales[0](0, cols), grouped[:])
-                        first_layer(accs[0], words[0], scales[0], e, 0, range(2 * q, 2 * q + 2))
-                    continue
-                if i == 0:
-                    grouped = turn.tile([P, H, J], BF16, name="first", align_bytes=64)
-                elif i == 2 * G - 2:
-                    grouped = ends.tile([P, H, J], BF16, name="fifth", offset=0, align_bytes=64)
-                elif share[i]:
-                    grouped = vector_ring([P, H, J], BF16)
-                else:
-                    grouped = scalar_ring()
-                interleave(grouped[:], rows, share[i])
-                if pending:
-                    finish(*pending)
-                pending = (which, g, grouped[:])
-                if i == 1 and e > 0:
-                    way_back(e - 1, banks, gates, turn.tile([P, NB, C], F32, name="gated", align_bytes=64))
-
-            g = G - 1
-            tail = ring_tile(3 * e + 2, [P, J * N + NB * C], name="tail", start=4 * J * H)
-            if loaded < G:
-                chunk = ring_tile(3 * e + 2, [P, J * H])[:]
-                width = J * H // parts
-                for q in range(parts):
-                    nc.sync.dma_start(chunk[:, q * width:(q + 1) * width], w_rows[1][e, :, g, q * width:(q + 1) * width])
-            else:
-                chunk = raw[:, g]
-            raw2 = tail[:, :J * N]
-            nc.sync.dma_start(raw2, w2_rows[:, e])
-            if e == 0:
-                nc.sync.dma_start(gates_early[:], gate_rows[:, :, :S - C])
+                if i == G - 1:
+                    for q in range(parts):
+                        sil = work.tile([P, C, pair], F32, name="sil", align_bytes=64)
+                        nc.scalar.activation(sil[:], accs[0][0][:, q * pair:(q + 1) * pair, :].rearrange("p t c -> p c t"), SILU)
+                        sils.append(sil)
             if last:
-                gates = tail[:, J * N:].rearrange("p (b s) -> p b s", b=NB)
-                nc.sync.dma_start(gates, gate_rows[:, :, S - C:])
-            else:
-                gates = gates_early[:, :, C * e:C * e + C]
-            grouped = vector_ring([P, H + N, J], BF16)
-            if last:
-                src = chunk.rearrange("p (j m t) -> p m t j", j=J, t=TILES)
-                dst = grouped[:, :H].rearrange("p (t m) j -> p m t j", t=TILES)
-                m = share[-1]
-                nc.vector.tensor_copy(dst[:, :m, :, :2], src[:, :m, :, :2])
-                nc.scalar.copy(dst[:, m:, :, :2], src[:, m:, :, :2])
-                finish(*pending)
+                g = G - 1
+                grouped = staging()
+                dst = grouped[:].rearrange("p (t m) j -> p m t j", t=TILES)
+                rows = J * H // 2
+                srcs = [load(w_rows[1][e, :, g, q * rows:(q + 1) * rows], [P, rows])[:].rearrange("p (v m t) -> p m t v", v=2, t=TILES)
+                        for q in range(2)]
+                nc.vector.tensor_copy(dst[:, :EVEN_SHARE, :, :2], srcs[0][:, :EVEN_SHARE])
+                nc.scalar.copy(dst[:, EVEN_SHARE:, :, :2], srcs[0][:, EVEN_SHARE:])
                 for t in range(2):
-                    nc.vector.tensor_copy(dst[:, :, t, 2:], src[:, :, t, 2:])
-                nc.scalar.copy(dst[:, :, 2:, 2:], src[:, :, 2:, 2:])
-            else:
-                interleave(grouped[:, :H], chunk, share[-1])
-                finish(*pending)
-            pair = TILES // parts
+                    nc.vector.tensor_copy(dst[:, :, t, 2:], srcs[1][:, :, t])
+                nc.scalar.copy(dst[:, :, 2:, 2:], srcs[1][:, :, 2:])
+                for t in range(TILES):
+                    cols = slice(t * P, t * P + P)
+                    quantise(words[1][:, g, cols], scales[1](g, cols), grouped[:, cols, :])
+                    first_layer(accs[1], words[1], scales[1], e, g, [t])
             if last:
-                sils = [ring_tile(3 * e + 1, [P, C, pair], name=f"sil{q}_", start=4 * C * pair * q, align=64) for q in range(parts)]
+                raws = [load(w2_rows[:, late], [P, J * N]) for late in range(E - LATE, E)]
+                states = [w2_tiles() for late in range(LATE)]
+                first = keep.tile([P, P, J], BF16, name="first_block", align_bytes=64)
+                src = raws[0][:].rearrange("p (j c i) -> p c j i", j=J, i=LINE)
+                nc.scalar.copy(first[:].rearrange("p (c i) j -> p c j i", i=LINE), src[:, :P // LINE])
+                w2_interleave(raws[0], [1], states[0])
+                quantise(states[0][1][:, :P], states[0][2][:, :P], first[:])
+                hidden = keep.tile([P, C, TILES], BF16, name="first_block", align_bytes=64)
             else:
-                sils = [ends.tile([P, C, pair], F32, name="sil", offset=0, align_bytes=64)]
-            for q in range(parts):
-                nc.scalar.activation(sils[q][:], accs[0][0][:, q * pair:(q + 1) * pair, :].rearrange("p t c -> p c t"), SILU)
-            if last:
-                w2_grouped = [ends.tile([P, P, J], BF16, name=f"w2_grouped{b}", offset=2 * J * (H + P * b), align_bytes=64)[:] for b in range(NB)]
-            else:
-                w2_grouped = [grouped[:, H:]]
-            src = raw2.rearrange("p (j c i) -> p c j i", j=J, i=LINE)
-            width = N // LINE // parts
-            for q in range(parts):
-                nc.scalar.copy(w2_grouped[q].rearrange("p (c i) j -> p c j i", i=LINE), src[:, q * width:(q + 1) * width])
-            steps = TILES if last else 1
-            for q in range(steps):
-                cols = slice(q * H // steps, (q + 1) * H // steps)
-                quantise(words[1][:, g, cols], scales[1](g, cols), grouped[:, cols, :])
-                first_layer(accs[1], words[1], scales[1], e, g, range(q * TILES // steps, (q + 1) * TILES // steps))
-
-            w2_scales = work.tile([P, N], U8, name="w2_scales", align_bytes=64)
-            hidden = turn.tile([P, C, TILES], BF16, name="hidden", align_bytes=64)
-            if last:
-                h_words = ends.tile([P, C], U32, name="h_words_last", offset=2 * J * H, align_bytes=64)
-            else:
-                h_words = work.tile([P, C], U32, name="h_words", align_bytes=64)
-            h_scales = work.tile([P, C], U8, name="h_scales", align_bytes=64)
-            if not last:
-                w2_words = work.tile([P, N], U32, name="w2_words", align_bytes=64)
-                w2_blocks = [w2_words[:, P * b:P * b + P] for b in range(NB)]
-                quantise(w2_words[:], w2_scales[:], grouped[:, H:])
+                hidden = work.tile([P, C, TILES], BF16, name="hidden", align_bytes=64)
             for q in range(parts):
                 nc.vector.tensor_tensor(
                     hidden[:, :, q * pair:(q + 1) * pair], sils[q][:], accs[1][q][:].rearrange("p t c -> p c t"), MULT
                 )
             if last:
-                block0 = ring_tile(3 * e + 1, [P, P], U32, name="block0_")
-                quantise(block0[:], w2_scales[:, :P], w2_grouped[0])
-            quantise(h_words[:], h_scales[:], hidden[:])
-            if last:
-                block1 = turn.tile([P, P], U32, name="hidden", align_bytes=64)
-                quantise(block1[:], w2_scales[:, P:], w2_grouped[1])
-                w2_blocks = [block0[:], block1[:]]
-            banks = [psum.tile([P, NB // parts, C], F32, name="y") for q in range(parts)]
-            for b in range(NB):
-                nc.tensor.matmul_mx(
-                    out=banks[b * parts // NB][:, b % (NB // parts), :],
-                    lhsT=w2_blocks[b].bitcast(FP8X4),
-                    lhsT_scale=w2_scales[:, P * b:P * b + P],
-                    rhs=h_words[:].bitcast(FP8X4),
-                    rhs_scale=h_scales[:],
-                    start=True,
-                    stop=True,
-                )
-        way_back(E - 1, banks, gates, ends.tile([P, NB, C], F32, name="gated_last", offset=2 * J * (H + P), align_bytes=64))
-        for b in range(NB):
+                w2_quantise([1], states[0])
+                h_words = ring.tile([P, C], U32, name="h_words_last", offset=ends[-2] - BURST, align_bytes=64)
+            else:
+                h_words = keep.tile([P, C], U32, name=f"h_words{e}", align_bytes=64)
+            hq = (h_words, keep.tile([P, C], U8, name=f"h_scales{e}", align_bytes=64))
+            quantise(hq[0][:], hq[1][:], hidden[:])
+            hidden_codes.append(hq)
+            if e < E - LATE:
+                raw2 = load(w2_rows[:, e], [P, J * N])
+                if e == 0:
+                    nc.sync.dma_start(gates_early[:], gate_rows[:, :, :early])
+                state = w2_tiles()
+                w2_interleave(raw2, both, state)
+                w2_quantise(both, state)
+                gated = gated_sums(second_layer(state, hq, both), gates_early[:, :, C * e:C * e + C], both)
+                for b in both:
+                    scatter(e, b, gated[:, b, :])
+
+        last_raw = ends[-1] - BURST
+        gates = load(gate_rows[:, :, early:], [P, NB, S - early])
+        sums = [second_layer(states[0], hidden_codes[E - 2], [b]) for b in both]
+        for b in both:
+            w2_interleave(raws[1], [b], states[1])
+        scatter(E - 2, 0, gated_sums(sums[0], gates[:, :, :C], [0])[:, 0, :], on_scalar=True)
+        for b in both:
+            w2_quantise([b], states[1])
+        sums += [second_layer(states[1], hidden_codes[E - 1], [b]) for b in both]
+        gated = []
+        for q in range(1, 4):
+            e, b = divmod(q, NB)
+            late = ring.tile([P, C], F32, name=f"late{q}", offset=last_raw + 4 * C * q, align_bytes=64)
+            nc.vector.tensor_tensor(late[:], sums[q][:, 0, :], gates[:, b, C * e:C * e + C], MULT)
+            gated.append(late)
+        scatter(E - 2, 1, gated[0][:], on_scalar=True)
+        for b in both:
+            scatter(E - 1, b, gated[1 + b][:])
+        for b in both:
             nc.sync.dma_start(out[P * b:P * b + P, :], wins[b][:])

@@ -24,7 +24,7 @@ COPY = mybir.ActivationFunctionType.Copy
 LATE = 2
 BURST = 4096
 RING_BYTES = 16 * BURST
-SHARE = 48
+SHARE = 60
 EVEN_SHARE = 80
 
 FLOPS = 2 * S * (2 * K * H + H * N)

@@ -35,6 +35,7 @@ def tile_routed_moe_kernel(tc, xT, w1, w3, w2, gate, offs, out):
     x_rows = xT.rearrange("(g p j) n -> p g (j n)", p=P, j=J)
     w_rows = [w.rearrange("e (g p j) h -> e p g (j h)", p=P, j=J) for w in (w1, w3)]
     w2_rows = w2.rearrange("e (p j) n -> p e (j n)", j=J)
+    w2_blocks = w2.rearrange("e (p j) n -> p e j n", j=J)
     gate_rows = gate.rearrange("(b p) s -> p b s", p=P)
 
     with ExitStack() as ctx:
@@ -149,6 +150,36 @@ def tile_routed_moe_kernel(tc, xT, w1, w3, w2, gate, offs, out):
             else:
                 nc.vector.tensor_copy(window, values)
 
+        def block_interleave(late, b):
+            grouped = keep.tile([P, P, J], BF16, name=f"late_grouped{late}{b}", align_bytes=64)
+            nc.scalar.copy(grouped[:].rearrange("p (c i) j -> p c j i", i=LINE), raws[late, b][:].rearrange("p j (c i) -> p c j i", i=LINE))
+            codes[late, b] = grouped
+
+        def block_quantise(late, b):
+            block_words = keep.tile([P, P], U32, name=f"late_words{late}{b}", align_bytes=64)
+            block_scales = keep.tile([P, P], U8, name=f"late_scales{late}{b}", align_bytes=64)
+            quantise(block_words[:], block_scales[:], codes[late, b][:])
+            codes[late, b] = (None, block_words, block_scales)
+
+        def block_sums(late, b):
+            bank = psum.tile([P, C], F32, name="y", bufs=4)
+            hq = hidden_codes[E - LATE + late]
+            nc.tensor.matmul_mx(
+                out=bank[:],
+                lhsT=codes[late, b][1][:].bitcast(FP8X4),
+                lhsT_scale=codes[late, b][2][:],
+                rhs=hq[0][:].bitcast(FP8X4),
+                rhs_scale=hq[1][:],
+                start=True,
+                stop=True,
+            )
+            return bank
+
+        def late_gated(late, b, bank, start):
+            gated = ring.tile([P, C], F32, name=f"late{late}{b}", offset=start, align_bytes=64)
+            nc.vector.tensor_tensor(gated[:], bank[:], gates[b][:, C * late:C * late + C], MULT)
+            return gated
+
         hidden_codes = []
         both = range(NB)
         for e in range(E):
@@ -197,14 +228,17 @@ def tile_routed_moe_kernel(tc, xT, w1, w3, w2, gate, offs, out):
                     quantise(words[1][:, g, cols], scales[1](g, cols), grouped[:, cols, :])
                     first_layer(accs[1], words[1], scales[1], e, g, [t])
             if last:
-                raws = [load(w2_rows[:, late], [P, J * N]) for late in range(E - LATE, E)]
-                states = [w2_tiles() for late in range(LATE)]
-                first = keep.tile([P, P, J], BF16, name="first_block", align_bytes=64)
-                src = raws[0][:].rearrange("p (j c i) -> p c j i", j=J, i=LINE)
-                nc.scalar.copy(first[:].rearrange("p (c i) j -> p c j i", i=LINE), src[:, :P // LINE])
-                w2_interleave(raws[0], [1], states[0])
-                quantise(states[0][1][:, :P], states[0][2][:, :P], first[:])
-                hidden = keep.tile([P, C, TILES], BF16, name="first_block", align_bytes=64)
+                raws, starts, gates, codes = {}, {}, [], {}
+                for b in both:
+                    for late in range(LATE):
+                        raws[late, b] = load(w2_blocks[:, E - LATE + late, :, P * b:P * b + P], [P, J, P])
+                        starts[late, b] = ends[-1] - BURST
+                    gates.append(load(gate_rows[:, b, early:], [P, S - early]))
+                for late in range(LATE):
+                    block_interleave(late, 0)
+                for late in range(LATE):
+                    block_quantise(late, 0)
+                hidden = ring.tile([P, C, TILES], BF16, name="hidden_last", offset=starts[1, 0], align_bytes=64)
             else:
                 hidden = work.tile([P, C, TILES], BF16, name="hidden", align_bytes=64)
             for q in range(parts):
@@ -212,8 +246,10 @@ def tile_routed_moe_kernel(tc, xT, w1, w3, w2, gate, offs, out):
                     hidden[:, :, q * pair:(q + 1) * pair], sils[q][:], accs[1][q][:].rearrange("p t c -> p c t"), MULT
                 )
             if last:
-                w2_quantise([1], states[0])
-                h_words = ring.tile([P, C], U32, name="h_words_last", offset=ends[-2] - BURST, align_bytes=64)
+                for late in range(LATE):
+                    block_interleave(late, 1)
+                first_gated = late_gated(0, 0, block_sums(0, 0), starts[0, 1])
+                h_words = ring.tile([P, C], U32, name="h_words_last", offset=starts[0, 1] + 4 * C, align_bytes=64)
             else:
                 h_words = keep.tile([P, C], U32, name=f"h_words{e}", align_bytes=64)
             hq = (h_words, keep.tile([P, C], U8, name=f"h_scales{e}", align_bytes=64))
@@ -230,23 +266,14 @@ def tile_routed_moe_kernel(tc, xT, w1, w3, w2, gate, offs, out):
                 for b in both:
                     scatter(e, b, gated[:, b, :])
 
-        last_raw = ends[-1] - BURST
-        gates = load(gate_rows[:, :, early:], [P, NB, S - early])
-        sums = [second_layer(states[0], hidden_codes[E - 2], [b]) for b in both]
-        for b in both:
-            w2_interleave(raws[1], [b], states[1])
-        scatter(E - 2, 0, gated_sums(sums[0], gates[:, :, :C], [0])[:, 0, :], on_scalar=True)
-        for b in both:
-            w2_quantise([b], states[1])
-        sums += [second_layer(states[1], hidden_codes[E - 1], [b]) for b in both]
-        gated = []
-        for q in range(1, 4):
-            e, b = divmod(q, NB)
-            late = ring.tile([P, C], F32, name=f"late{q}", offset=last_raw + 4 * C * q, align_bytes=64)
-            nc.vector.tensor_tensor(late[:], sums[q][:, 0, :], gates[:, b, C * e:C * e + C], MULT)
-            gated.append(late)
-        scatter(E - 2, 1, gated[0][:], on_scalar=True)
-        for b in both:
-            scatter(E - 1, b, gated[1 + b][:])
+        last_sums = block_sums(1, 0)
+        for late in range(LATE):
+            block_quantise(late, 1)
+        scatter(E - 2, 0, first_gated[:], on_scalar=True)
+        sums = [block_sums(late, 1) for late in range(LATE)]
+        last_gated = late_gated(1, 0, last_sums, starts[1, 1])
+        scatter(E - 2, 1, late_gated(0, 1, sums[0], starts[1, 1] + 4 * C)[:], on_scalar=True)
+        scatter(E - 1, 0, last_gated[:])
+        scatter(E - 1, 1, late_gated(1, 1, sums[1], starts[0, 1])[:], on_scalar=True)
         for b in both:
             nc.sync.dma_start(out[P * b:P * b + P, :], wins[b][:])

@@ -150,9 +150,9 @@ def tile_routed_moe_kernel(tc, xT, w1, w3, w2, gate, offs, out):
             else:
                 nc.vector.tensor_copy(window, values)
 
-        def block_interleave(late, b):
+        def block_interleave(late, b, copy=nc.scalar.copy):
             grouped = keep.tile([P, P, J], BF16, name=f"late_grouped{late}{b}", align_bytes=64)
-            nc.scalar.copy(grouped[:].rearrange("p (c i) j -> p c j i", i=LINE), raws[late, b][:].rearrange("p j (c i) -> p c j i", i=LINE))
+            copy(grouped[:].rearrange("p (c i) j -> p c j i", i=LINE), raws[late, b][:].rearrange("p j (c i) -> p c j i", i=LINE))
             codes[late, b] = grouped
 
         def block_quantise(late, b):
@@ -214,19 +214,19 @@ def tile_routed_moe_kernel(tc, xT, w1, w3, w2, gate, offs, out):
             if last:
                 g = G - 1
                 grouped = staging()
-                dst = grouped[:].rearrange("p (t m) j -> p m t j", t=TILES)
-                rows = J * H // 2
-                srcs = [load(w_rows[1][e, :, g, q * rows:(q + 1) * rows], [P, rows])[:].rearrange("p (v m t) -> p m t v", v=2, t=TILES)
-                        for q in range(2)]
-                nc.vector.tensor_copy(dst[:, :EVEN_SHARE, :, :2], srcs[0][:, :EVEN_SHARE])
-                nc.scalar.copy(dst[:, EVEN_SHARE:, :, :2], srcs[0][:, EVEN_SHARE:])
-                for t in range(2):
-                    nc.vector.tensor_copy(dst[:, :, t, 2:], srcs[1][:, :, t])
-                nc.scalar.copy(dst[:, :, 2:, 2:], srcs[1][:, :, 2:])
-                for t in range(TILES):
-                    cols = slice(t * P, t * P + P)
-                    quantise(words[1][:, g, cols], scales[1](g, cols), grouped[:, cols, :])
-                    first_layer(accs[1], words[1], scales[1], e, g, [t])
+                columns = w_rows[1][e, :, g].rearrange("p (j h) -> p j h", j=J)
+                dst = grouped[:].rearrange("p (t m) (u v) -> p t m u v", t=TILES, v=2)
+                for q in range(2):
+                    raw = load(columns[:, :, q * H // 2:(q + 1) * H // 2], [P, J, H // 2])
+                    src = raw[:].rearrange("p (u v) (m t) -> p t m u v", v=2, t=TILES)
+                    ms = slice(q * P // 2, (q + 1) * P // 2)
+                    for copy, tiles in ((nc.vector.tensor_copy, slice(0, 2)), (nc.scalar.copy, slice(2, 4))):
+                        copy(dst[:, tiles, ms].rearrange("p t m u v -> p m u t v"), src[:, tiles].rearrange("p t m u v -> p m u t v"))
+                    for t in range(TILES):
+                        cols = slice(t * P + ms.start, t * P + ms.stop)
+                        quantise(words[1][:, g, cols], scales[1](g, cols), grouped[:, cols, :])
+                        if q == 1:
+                            first_layer(accs[1], words[1], scales[1], e, g, [t])
             if last:
                 raws, starts, gates, codes = {}, {}, [], {}
                 for b in both:
@@ -234,8 +234,8 @@ def tile_routed_moe_kernel(tc, xT, w1, w3, w2, gate, offs, out):
                         raws[late, b] = load(w2_blocks[:, E - LATE + late, :, P * b:P * b + P], [P, J, P])
                         starts[late, b] = ends[-1] - BURST
                     gates.append(load(gate_rows[:, b, early:], [P, S - early]))
-                for late in range(LATE):
-                    block_interleave(late, 0)
+                block_interleave(0, 0)
+                block_interleave(1, 0, nc.vector.tensor_copy)
                 for late in range(LATE):
                     block_quantise(late, 0)
                 hidden = ring.tile([P, C, TILES], BF16, name="hidden_last", offset=starts[1, 0], align_bytes=64)
@@ -273,7 +273,8 @@ def tile_routed_moe_kernel(tc, xT, w1, w3, w2, gate, offs, out):
         sums = [block_sums(late, 1) for late in range(LATE)]
         last_gated = late_gated(1, 0, last_sums, starts[1, 1])
         scatter(E - 2, 1, late_gated(0, 1, sums[0], starts[1, 1] + 4 * C)[:], on_scalar=True)
+        second_gated = late_gated(1, 1, sums[1], starts[1, 1] + 8 * C)
         scatter(E - 1, 0, last_gated[:])
-        scatter(E - 1, 1, late_gated(1, 1, sums[1], starts[0, 1])[:], on_scalar=True)
+        scatter(E - 1, 1, second_gated[:])
         for b in both:
             nc.sync.dma_start(out[P * b:P * b + P, :], wins[b][:])

from contextlib import ExitStack

import concourse.mybir as mybir

K, T, E, C, H, N = 1536, 1024, 4, 128, 512, 256
S = E * C
P = 128
J = 4
G = K // (P * J)
NB = N // P
TILES = H // P
LINE = 4

F32 = mybir.dt.float32
BF16 = mybir.dt.bfloat16
U32 = mybir.dt.uint32
U16 = mybir.dt.uint16
U8 = mybir.dt.uint8
FP8X4 = mybir.dt.float8_e4m3fn_x4
MULT = mybir.AluOpType.mult
SILU = mybir.ActivationFunctionType.Silu
COPY = mybir.ActivationFunctionType.Copy

LATE = 2
BURST = 4096
RING_BYTES = 16 * BURST
SHARE = 60
EVEN_SHARE = 80

FLOPS = 2 * S * (2 * K * H + H * N)


def tile_routed_moe_kernel(tc, xT, w1, w3, w2, gate, offs, out):
    nc = tc.nc
    x_rows = xT.rearrange("(g p j) n -> p g (j n)", p=P, j=J)
    w_rows = [w.rearrange("e (g p j) h -> e p g (j h)", p=P, j=J) for w in (w1, w3)]
    w2_rows = w2.rearrange("e (p j) n -> p e (j n)", j=J)
    w2_blocks = w2.rearrange("e (p j) n -> p e j n", j=J)
    gate_rows = gate.rearrange("(b p) s -> p b s", p=P)

    with ExitStack() as ctx:
        keep = ctx.enter_context(tc.tile_pool(name="keep", bufs=1))
        ring = ctx.enter_context(tc.tile_pool(name="ring", bufs=1))
        work = ctx.enter_context(tc.tile_pool(name="work", bufs=2))
        psum = ctx.enter_context(tc.psum_pool(name="psum", bufs=2))

        ends = [0]

        def load(source, shape):
            size = -(-4 * shape[1] * (shape[2] if len(shape) > 2 else 1) // BURST) * BURST
            start = ends[-1] if ends[-1] + size <= RING_BYTES else 0
            ends.append(start + size)
            raw = ring.tile(shape, F32, name=f"raw{len(ends)}", offset=start, align_bytes=BURST)
            nc.sync.dma_start(raw[:], source)
            return raw

        def quantise(words, scales, grouped):
            nc.vector.quantize_mx(out=words.bitcast(FP8X4), scales=scales, in_=grouped.rearrange("p c j -> p (c j)"))

        def staging():
            return work.tile([P, H, J], BF16, name="staging", bufs=6, align_bytes=64)

        wins = []
        for b in range(NB):
            win = keep.tile([P, T], F32, name=f"win{b}", align_bytes=BURST)
            nc.vector.memset(win[:], 0.0)
            wins.append(win)
        lst = keep.tile([P, S // 16], U16, name="lst")

        slot_words = keep.tile([P, G, S], U32, name="slot_words", align_bytes=64)
        slot_scales = keep.tile([P, S], U8, name="slot_scales", align_bytes=64)
        token_scales = keep.tile([P, T], U8, name="token_scales", align_bytes=64)
        half = T // 2
        for g in range(G):
            xraw = load(x_rows[:, g], [P, J * T])
            if g == 0:
                nc.sync.dma_start(lst[:], offs)
            token_words = work.tile([P, T], U32, name="token_words", align_bytes=64)
            src = xraw[:].rearrange("p (j c i) -> p c j i", j=J, i=LINE)
            for u, copy in enumerate((nc.vector.tensor_copy, nc.scalar.copy)):
                grouped = staging()
                copy(grouped[:].rearrange("p (c i) j -> p c j i", i=LINE), src[:, u * half // LINE:(u + 1) * half // LINE])
                tokens = slice(u * half, (u + 1) * half)
                quantise(token_words[:, tokens], token_scales[4 * g:, tokens], grouped[:])
            nc.vector.tensor_copy(slot_words[:, g, :], token_words[:].indirect(lst[:]))
        nc.vector.tensor_copy(slot_scales[:], token_scales[:].indirect(lst[:]))

        early = (E - LATE) * C
        gates_early = keep.tile([P, NB, early], F32, name="gates_early", align_bytes=256)

        def first_layer(accs, words, scales, e, g, tiles):
            per_bank = TILES // len(accs)
            for t in tiles:
                nc.tensor.matmul_mx(
                    out=accs[t // per_bank][:, t % per_bank, :],
                    lhsT=words[:, g, P * t:P * t + P].bitcast(FP8X4),
                    lhsT_scale=scales(g, slice(P * t, P * t + P)),
                    rhs=slot_words[:, g, C * e:C * e + C].bitcast(FP8X4),
                    rhs_scale=slot_scales[4 * g:, C * e:C * e + C],
                    start=(g == 0 and t % per_bank == 0),
                    stop=(g == G - 1 and t % per_bank == per_bank - 1),
                )

        def interleave(grouped, raw, m):
            src = raw.rearrange("p (u v m t) -> p m u t v", u=2, v=2, t=TILES)
            dst = grouped.rearrange("p (t m) (u v) -> p m u t v", t=TILES, v=2)
            if m:
                nc.vector.tensor_copy(dst[:, :m], src[:, :m])
            if m < P:
                nc.scalar.copy(dst[:, m:], src[:, m:])

        def w2_interleave(raw, blocks, state, copy=nc.scalar.copy):
            cols = slice(P * blocks[0], P * blocks[-1] + P)
            src = raw[:].rearrange("p (j c i) -> p c j i", j=J, i=LINE)
            copy(state[0][:, cols].rearrange("p (c i) j -> p c j i", i=LINE), src[:, cols.start // LINE:cols.stop // LINE])

        def w2_quantise(blocks, state):
            grouped, words, scales = state
            cols = slice(P * blocks[0], P * blocks[-1] + P)
            quantise(words[:, cols], scales[:, cols], grouped[:, cols])

        def w2_tiles():
            return (work.tile([P, N, J], BF16, name="w2_grouped", align_bytes=64),
                    work.tile([P, N], U32, name="w2_words", align_bytes=64),
                    work.tile([P, N], U8, name="w2_scales", align_bytes=64))

        def second_layer(state, hq, blocks):
            bank = psum.tile([P, len(blocks), C], F32, name="y", bufs=4)
            for q, b in enumerate(blocks):
                nc.tensor.matmul_mx(
                    out=bank[:, q, :],
                    lhsT=state[1][:, P * b:P * b + P].bitcast(FP8X4),
                    lhsT_scale=state[2][:, P * b:P * b + P],
                    rhs=hq[0][:].bitcast(FP8X4),
                    rhs_scale=hq[1][:],
                    start=True,
                    stop=True,
                )
            return bank

        def gated_sums(bank, gates, blocks):
            gated = work.tile([P, len(blocks), C], F32, name="gated", bufs=4, align_bytes=64)
            nc.vector.tensor_tensor(gated[:], bank[:], gates[:, blocks[0]:blocks[-1] + 1, :], MULT)
            return gated

        def scatter(e, b, values, on_scalar=False):
            window = wins[b][:].indirect(lst[:, e * C // 16:(e + 1) * C // 16])
            if on_scalar:
                nc.scalar.activation(window, values, COPY)
            else:
                nc.vector.tensor_copy(window, values)

        def block_interleave(late, b, copy=nc.scalar.copy):
            grouped = keep.tile([P, P, J], BF16, name=f"late_grouped{late}{b}", align_bytes=64)
            copy(grouped[:].rearrange("p (c i) j -> p c j i", i=LINE), raws[late, b][:].rearrange("p j (c i) -> p c j i", i=LINE))
            codes[late, b] = grouped

        def block_quantise(late, b):
            block_words = keep.tile([P, P], U32, name=f"late_words{late}{b}", align_bytes=64)
            block_scales = keep.tile([P, P], U8, name=f"late_scales{late}{b}", align_bytes=64)
            quantise(block_words[:], block_scales[:], codes[late, b][:])
            codes[late, b] = (None, block_words, block_scales)

        def block_sums(late, b):
            bank = psum.tile([P, C], F32, name="y", bufs=4)
            hq = hidden_codes[E - LATE + late]
            nc.tensor.matmul_mx(
                out=bank[:],
                lhsT=codes[late, b][1][:].bitcast(FP8X4),
                lhsT_scale=codes[late, b][2][:],
                rhs=hq[0][:].bitcast(FP8X4),
                rhs_scale=hq[1][:],
                start=True,
                stop=True,
            )
            return bank

        def late_gated(late, b, bank, start):
            gated = ring.tile([P, C], F32, name=f"late{late}{b}", offset=start, align_bytes=64)
            nc.vector.tensor_tensor(gated[:], bank[:], gates[b][:, C * late:C * late + C], MULT)
            return gated

        hidden_codes = []
        both = range(NB)
        for e in range(E):
            last = e == E - 1
            parts = 1
            pair = TILES // parts
            accs = [[psum.tile([P, TILES, C], F32, name="acc0", bufs=1)],
                    [psum.tile([P, pair, C], F32, name=f"acc{1 + q}", bufs=2 - q) for q in range(parts)]]
            words = [work.tile([P, G, H], U32, name=f"words{which}", align_bytes=64) for which in range(2)]
            planes = [work.tile([P, G, H], U8, name=f"scales{which}", align_bytes=64) for which in range(2)]
            scales = [lambda g, cols: planes[0][:, g, cols], lambda g, cols: planes[1][:, g, cols]]
            if last:
                scales[1] = lambda g, cols: planes[1][4 * (g % 2):, g // 2, cols]
            sils = []
            for i in range(2 * G - (1 if last else 0)):
                which, g = divmod(i, G)
                raw = load(w_rows[which][e, :, g], [P, J * H])
                grouped = staging()
                share = 0 if (e == 0 and i < 2) else EVEN_SHARE if (last and i == 2 * G - 2) else SHARE
                interleave(grouped[:], raw[:], share)
                quantise(words[which][:, g], scales[which](g, slice(0, H)), grouped[:])
                if last and which == 1:
                    for back in range(2 * g):
                        first_layer(accs[which], words[which], scales[which], e, back, range(TILES))
                else:
                    first_layer(accs[which], words[which], scales[which], e, g, range(TILES))
                if i == G - 1:
                    for q in range(parts):
                        sil = work.tile([P, C, pair], F32, name="sil", align_bytes=64)
                        nc.scalar.activation(sil[:], accs[0][0][:, q * pair:(q + 1) * pair, :].rearrange("p t c -> p c t"), SILU)
                        sils.append(sil)
            if last:
                g = G - 1
                grouped = staging()
                columns = w_rows[1][e, :, g].rearrange("p (j h) -> p j h", j=J)
                dst = grouped[:].rearrange("p (t m) (u v) -> p t m u v", t=TILES, v=2)
                for q in range(2):
                    raw = load(columns[:, :, q * H // 2:(q + 1) * H // 2], [P, J, H // 2])
                    src = raw[:].rearrange("p (u v) (m t) -> p t m u v", v=2, t=TILES)
                    ms = slice(q * P // 2, (q + 1) * P // 2)
                    for copy, tiles in ((nc.vector.tensor_copy, slice(0, 2)), (nc.scalar.copy, slice(2, 4))):
                        copy(dst[:, tiles, ms].rearrange("p t m u v -> p m u t v"), src[:, tiles].rearrange("p t m u v -> p m u t v"))
                    for t in range(TILES):
                        cols = slice(t * P + ms.start, t * P + ms.stop)
                        quantise(words[1][:, g, cols], scales[1](g, cols), grouped[:, cols, :])
                        if q == 1:
                            first_layer(accs[1], words[1], scales[1], e, g, [t])
            if last:
                raws, starts, gates, codes = {}, {}, [], {}
                for b in both:
                    for late in range(LATE):
                        raws[late, b] = load(w2_blocks[:, E - LATE + late, :, P * b:P * b + P], [P, J, P])
                        starts[late, b] = ends[-1] - BURST
                    gates.append(load(gate_rows[:, b, early:], [P, S - early]))
                block_interleave(0, 0)
                block_interleave(1, 0, nc.vector.tensor_copy)
                for late in range(LATE):
                    block_quantise(late, 0)
                hidden = ring.tile([P, C, TILES], BF16, name="hidden_last", offset=starts[1, 0], align_bytes=64)
            else:
                hidden = work.tile([P, C, TILES], BF16, name="hidden", align_bytes=64)
            for q in range(parts):
                nc.vector.tensor_tensor(
                    hidden[:, :, q * pair:(q + 1) * pair], sils[q][:], accs[1][q][:].rearrange("p t c -> p c t"), MULT
                )
            if last:
                for late in range(LATE):
                    block_interleave(late, 1)
                first_gated = late_gated(0, 0, block_sums(0, 0), starts[0, 1])
                h_words = ring.tile([P, C], U32, name="h_words_last", offset=starts[0, 1] + 4 * C, align_bytes=64)
            else:
                h_words = keep.tile([P, C], U32, name=f"h_words{e}", align_bytes=64)
            hq = (h_words, keep.tile([P, C], U8, name=f"h_scales{e}", align_bytes=64))
            quantise(hq[0][:], hq[1][:], hidden[:])
            hidden_codes.append(hq)
            if e < E - LATE:
                raw2 = load(w2_rows[:, e], [P, J * N])
                if e == 0:
                    nc.sync.dma_start(gates_early[:], gate_rows[:, :, :early])
                state = w2_tiles()
                w2_interleave(raw2, both, state)
                w2_quantise(both, state)
                gated = gated_sums(second_layer(state, hq, both), gates_early[:, :, C * e:C * e + C], both)
                for b in both:
                    scatter(e, b, gated[:, b, :])

        last_sums = block_sums(1, 0)
        for late in range(LATE):
            block_quantise(late, 1)
        scatter(E - 2, 0, first_gated[:], on_scalar=True)
        sums = [block_sums(late, 1) for late in range(LATE)]
        last_gated = late_gated(1, 0, last_sums, starts[1, 1])
        scatter(E - 2, 1, late_gated(0, 1, sums[0], starts[1, 1] + 4 * C)[:], on_scalar=True)
        second_gated = late_gated(1, 1, sums[1], starts[1, 1] + 8 * C)
        scatter(E - 1, 0, last_gated[:])
        scatter(E - 1, 1, second_gated[:])
        for b in both:
            nc.sync.dma_start(out[P * b:P * b + P, :], wins[b][:])
